import numpy as np, ml_dtypes
CORES = [24,25,26,27,28,29,30,31]
N = 8
BF = ml_dtypes.bfloat16
def gentries(a):
    return np.ascontiguousarray(a.reshape(8, 16, -1).transpose(0, 2, 1)).reshape(8, -1)
def gtable(e):
    e = np.asarray(e); return np.ascontiguousarray(e.reshape(8, -1, 16).transpose(0, 2, 1)).reshape(128, -1).astype(np.int32)
W, SB, P, HOPS, STEP, GAIN = 2048, 11, 256, 4, 3, 16
def parts(rng):
    x = rng.integers(0, 64, (N, 8, 16, W)); n = rng.integers(0, W, (N, 8, 16, W))
    s = rng.integers(0, rng.integers(2, 9, (N, 8, 1, W)) + 1, (N, 8, 16, W))
    return x, n, s, rng.integers(0, W, (N, 8, P)), rng.integers(0, 64, (N, 8, 16, P)), rng.integers(1, 256, (N, 8, 16, 1))
def lonely(rng, n, s, v, old, few, start):
    for q in range(N):
        for g in range(8):
            o = rng.permutation(W); a = o[:old]; b = o[old:old + few]
            s[q, g][:, a] = 0; n[q, g][:, b] = a[rng.integers(0, old, (16, few))]
            v[q, g, rng.permutation(P)[:start]] = b[rng.integers(0, few, start)]
def scarce(rng, n, s, v):
    lone = np.zeros((N, 8), np.int64); sh = int(rng.integers(0, 4))
    for q in range(N):
        for g in range(8):
            a, b = [int(m) for m in rng.permutation(W)[:2]]
            n[q, g][:, a] = b; s[q, g][:, b] = 0; lone[q, g] = a
    live = np.any(np.take_along_axis(s, n, 3) > 0, axis=2)
    for q in range(N):
        for g in range(8):
            c = np.flatnonzero(live[q, g])
            v[q, g] = np.where(live[q, g, v[q, g]], v[q, g], c[rng.integers(0, len(c), P)])
        for m in rng.permutation(8 * P)[:(q + sh) & 3]:
            g = int(m) // P; v[q, g, int(m) - g * P] = lone[q, g]
def plant(rng, x, n, s, v, z):
    for q in range(N):
        for g in range(8):
            o = [int(m) for m in 1 + rng.permutation(W - 1)[:25]]; X, M, S, Z = x[q, g], n[q, g], s[q, g], z[q, g]
            a, b, c = o[:3]
            M[:, 0] = c; S[:, c] = 0; Z[:, 0] = 0; v[q, g, 0] = 0
            M[:, a] = b; M[:, b] = 0; S[:, b] = rng.integers(1, 9, 16); v[q, g, 1] = a
            for p, j in ((2, 3), (P - 1, 9)):
                a, b, c, d1, d2, d3 = o[j:j + 6]; r = 63 * rng.integers(0, 2, 16)
                Z[:, p] = r; v[q, g, p] = a; M[:, a] = c; M[0, a] = b
                S[:, b] = rng.integers(1, 9, 16); S[15, b] = 0; M[0, b] = d3
                S[:, c] = rng.integers(1, 9, 16); M[:, c] = d1; M[15, c] = d2
                X[:, d1] = r; X[:, d2] = r; X[:, d3] = r; X[15, d1] = r[15] ^ 1
            for p, j in ((3, 15), (P - 2, 20)):
                a, b, c, d, h = o[j:j + 5]; r = 63 * rng.integers(0, 2, 16); k = int(rng.integers(1, 16))
                Z[:, p] = r; v[q, g, p] = a; M[:, a] = c; M[0, a] = b
                S[:, b] = rng.integers(1, 9, 16); S[0, b] = 0; M[0, b] = d; X[:, d] = r
                S[:, c] = 0; S[k, c] = int(rng.integers(1, 9)); M[k, c] = h; X[:, h] = 63 - r
def pack(x, e, v, z, w):
    return {"xs": np.ascontiguousarray(x.reshape(N, 128, W)).astype(np.float32).astype(BF), "en": np.ascontiguousarray(e.reshape(N, 128, W)).astype(np.int32),
            "v0": np.stack([gtable(a) for a in v]), "z0": np.ascontiguousarray(z.reshape(N, 128, P)).astype(np.float32).astype(BF), "wt": np.ascontiguousarray(w.reshape(N, 128, 1)).astype(np.int32)}
def setup_inputs(rng):
    x, n, s, v, z, w = parts(rng)
    lonely(rng, n, s, v, W // 8, W // 16, P // 8)
    return pack(x, n + W * s, v, z, w)
def setup_inputs_spread(rng):
    x, n, s, v, z, w = parts(rng)
    ex = rng.choice(np.array([0.25, 1.0, 4.0]), (N, 8, 1, W)); es = rng.choice(np.array([0.25, 1.0, 4.0]), (N, 8, 1, W)); en = rng.choice(np.array([1.0, 3.0]), (N, 8, 1, W))
    x = (64 * rng.random(x.shape) ** ex).astype(np.int64); s = (9 * rng.random(x.shape) ** es).astype(np.int64); n = (W * rng.random(x.shape) ** en).astype(np.int64)
    x = np.minimum(x, 63); s = np.minimum(s, 8); n = np.minimum(n, W - 1)
    v = np.minimum((W * rng.random(v.shape) ** 2).astype(np.int64), W - 1)
    z = np.minimum((64 * rng.random(z.shape) ** rng.choice(np.array([0.25, 1.0, 4.0]), (N, 8, 1, P))).astype(np.int64), 63)
    w = np.minimum(1 + (255 * rng.random(w.shape) ** 4).astype(np.int64), 255)
    scarce(rng, n, s, v)
    return pack(x, n + W * s, v, z, w)
def setup_inputs_ends(rng):
    x, n, s, v, z, w = parts(rng); hi = 9 * W - 1
    x = 63 * rng.integers(0, 2, x.shape); z = 63 * rng.integers(0, 2, z.shape); w = 1 + 254 * rng.integers(0, 2, w.shape); v = (W - 1) * rng.integers(0, 2, v.shape)
    e = np.where(rng.random(x.shape) < 0.8, hi * rng.integers(0, 2, x.shape), rng.choice(np.array([1, W - 2, 8 * W, 8 * W + 1, 9 * W - 2]), x.shape))
    e[..., W - 1] = rng.choice(np.array([hi, hi, 8 * W + 1, 9 * W - 2]), (N, 8, 16)); e[:, :, 15, W - 1] = hi
    e[..., W - 3] = 0; e[:, 7, :, W - 4] = hi
    one = rng.integers(0, 16, (N, 8)); one[:, 7] = 15; one[N - 1] = 15
    e[..., 0] = np.where(np.arange(16) == one[..., None], hi, 0)
    full = 63 * rng.integers(0, 2, (N, 8, 1)); full[:, 7] = 63
    for c in (1, W - 2, W - 1): x[..., c] = full
    for p in (0, P - 1): z[..., p] = full
    for p in (1, P - 2, P - 3): z[..., p] = 63 - full
    for p in (0, 1, P - 2, P - 1): v[..., p] = W - 1
    v[..., 2] = 0; v[..., P - 3] = W - 3; w[:, 7] = 255; w[:, 0, 0] = 1
    return pack(x, e, v, z, w)
def setup_inputs_corners(rng):
    x, n, s, v, z, w = parts(rng); o = [int(a) for a in rng.permutation(8)]; col = np.arange(W); i = np.arange(16)[:, None]
    n[:, o[0]] = col
    k = rng.integers(0, 4, (N, 16, W))
    n[:, o[1]] = np.where(k == 0, 0, np.where(k == 1, W - 1, np.where(k == 2, col, (col + 1) & (W - 1))))
    h = P // 2; s[:, o[2]] = 0; w[:, o[2], 0] = 255; w[:, o[2], 1] = W // 256 - 1
    z[:, o[2], :, :h] = 0; z[:, o[2], 0, :h] = W // 256; z[:, o[2], 1, :h] = 1
    s[:, o[3]] = np.where(i < 8, i + 1, 0)
    s[:, o[4]] = np.where(i == 0, 4, np.where(i == 12, 6, np.where(i == 13, 8, 0)))
    s[:, o[5]] = np.where(i == 0, 4, np.where(i == 13, 8, 0))
    for c in (3, 4, 5): x[:, o[c]] = np.repeat(x[:, o[c], :, :1], W, axis=2)
    s[::2, o[6]] = 8; s[1::2, o[6]] = 0
    v[..., 0] = W - 1; v[..., 1] = 0; v[..., P - 1] = W - 1
    for q in range(N):
        m = rng.permutation(W - 1); a = np.append(m[:P - 1], W - 1); b = m[P - 1:2 * P - 1]
        n[q, o[7]][:, a] = b; n[q, o[7]][:, b] = b; s[q, o[7]][:, b] = rng.integers(1, 9, (16, P)); v[q, o[7]] = a
    return pack(x, n + W * s, v, z, w)
def setup_inputs_crowd(rng):
    x, n, s, v, z, w = parts(rng)
    lonely(rng, n, s, v, W // 4, W // 4, 1)
    want = (8 * P, 8 * P - 1, 255, 256); sh = int(rng.integers(0, 4))
    for q in range(N):
        bad = np.zeros(8 * P, bool); bad[rng.permutation(8 * P)[:want[(q + sh) % 4]]] = True; bad = bad.reshape(8, P)
        for g in range(8):
            a, b, c, d, hub = [int(m) for m in rng.permutation(W)[:5]]
            n[q, g, :, a] = b; s[q, g, :, b] = 8
            if g % 3 == 0: n[q, g, :, b] = a
            if g % 3 == 1: n[q, g, :, b] = hub
            n[q, g, :, c] = d; s[q, g, :, d] = 0
            v[q, g] = np.where(bad[g], c, a)
    z[:, ::2] = np.repeat(z[:, ::2, :, :1], P, axis=3)
    return pack(x, n + W * s, v, z, w)
def setup_inputs_ties(rng):
    x, n, s, v, z, w = parts(rng)
    base = rng.integers(0, 16, (N, 8, 16, 1)); proto = rng.integers(0, 4, (N, 8, W))
    x = np.repeat(base, W, axis=3); x[:, :, 0] = base[:, :, 0] + GAIN * proto
    i = np.arange(16)[:, None]; s = (i + rng.integers(0, 8, (N, 8, 1, W))) & 7
    s = np.where((rng.random((N, 8, 1, W)) < 0.5) & (s == 0) & (i < 8), 8, s)
    n = np.where(rng.random((N, 8, 1, W)) < 0.3, rng.integers(0, W, (N, 8, 1, W)), n)
    z[:, :, 0] = 63 * (rng.random((N, 8, P)) < 0.25)
    plant(rng, x, n, s, v, z)
    return pack(x, n + W * s, v, z, w)
def check_inputs(d):
    bad = []
    for k, lo, hi in (("xs", 0, 63), ("en", 0, 9 * W - 1), ("v0", 0, W - 1), ("z0", 0, 63), ("wt", 1, 255)):
        a = np.asarray(d[k]).astype(np.float64)
        if not (np.min(a) >= lo and np.max(a) <= hi): bad.append("range of " + k)
        elif np.any(a != np.floor(a)): bad.append("whole numbers of " + k)
    return bad
def reference(xs, en, v0, z0, wt):
    x = xs.astype(np.float32).astype(np.int64).reshape(N, 8, 16, W); e = en.astype(np.int64).reshape(N, 8, 16, W); w = wt.astype(np.int64).reshape(N, 8, 16, 1)
    v = np.stack([gentries(a) for a in v0]).astype(np.int64); z = z0.astype(np.float32).astype(np.int64).reshape(N, 8, 16, P)
    tau = np.zeros((N, 8, P), np.int64); A = np.zeros(N, np.int64); k16 = np.arange(16); pn = np.arange(P)
    qi = np.arange(N)[:, None, None]; gi = np.arange(8)[None, :, None]
    for t in range(HOPS):
        if t > 0: v = np.roll(v, STEP, axis=0); tau = np.roll(tau, STEP, axis=0); z = np.roll(z, STEP, axis=0)
        ring = np.take_along_axis(e, v[:, :, None, :], 3) & (W - 1)
        F = np.take_along_axis(e, ring.reshape(N, 8, 1, 16 * P), 3).reshape(N, 8, 16, 16, P)
        newer = np.count_nonzero((F >> SB) > tau[:, :, None, None, :], axis=2)
        fk = F[:, :, (k16 + t) & 15, k16]
        rec = np.take_along_axis(x, (fk & (W - 1)).reshape(N, 8, 1, 16 * P), 3).reshape(N, 8, 16, 16, P)
        score = np.add.reduce(np.abs(rec - z[:, :, :, None, :]), axis=2) - GAIN * newer
        ok = (k16[:, None] < 16 - tau[:, :, None, :]) & ((fk >> SB) > tau[:, :, None, :])
        best = np.argmin(np.where(ok, score, 2 ** 20), axis=2); found = np.any(ok, axis=2)
        fa = np.take_along_axis(fk, best[:, :, None, :], 2)[:, :, 0]
        u = np.add.reduce(w * z, axis=2) & (W - 1)
        f = np.where(found, fa & (W - 1), ((u * u >> 5) + 37 * u + A[:, None, None]) & (W - 1))
        tau = np.where(found, fa >> SB, 0)
        z = np.where(found[:, :, None, :], z, np.abs(z - np.take_along_axis(x, f[:, :, None, :], 3)))
        A = np.count_nonzero(np.logical_not(found), axis=(1, 2)) & 255
        first = np.full((N, 8, W), P, np.int64)
        np.minimum.at(first, (qi, gi, np.concatenate([v, f], axis=2)), np.concatenate([pn, pn])[None, None, :])
        stands = (f != v) & (np.take_along_axis(first, v, 2) == pn) & (np.take_along_axis(first, f, 2) == pn)
        q, g, p = np.nonzero(stands); a = v[q, g, p]; b = f[q, g, p]
        ca = e[q, g, :, a]; cb = e[q, g, :, b]
        na = np.where(k16 % 2 == 0, cb, ca); nb = np.where(k16 % 2 == 0, ca, cb)
        na[:, 15] = b + W * (9 + t); nb[:, 15] = a + W * (9 + t)
        e[q, g, :, a] = na; e[q, g, :, b] = nb
        v = f
    return {"ys": np.add.reduce(e * (k16[:, None] + 1), axis=2).astype(np.float32), "yp": (v + W * tau).astype(np.float32), "yz": z.reshape(N, 128, P).astype(np.float32).astype(BF)}

@@ -1,0 +1,588 @@
+import math
+from concourse.mybir import AluOpType as A, ActivationFunctionType as AF
+
+HOPS, STEP = 4, 3
+F32, BF, F16, I32, U16 = "float32", "bfloat16", "float16", "int32", "uint16"
+SB = {
+    "ENI": (2048, I32), "E": (2560, F32), "X": (2048, BF), "YT": (2560, F32), "V0": (16, I32), "WTI": (1, I32),
+    "F": (4096, F32), "CM": (4096, BF), "RW": (4096, BF), "MX": (4096, BF), "RH": (2048, BF),
+    "L": (2048, BF), "EXP": (512, BF), "Q0": (512, BF), "Q1": (128, F32), "Q2": (128, F32), "Q3": (128, F32), "Q4": (128, F32),
+    "PI": (4, I32), "COL": (42, F32), "I": (128, BF), "NI": (128, BF), "N2I": (128, BF), "BI": (128, BF), "I3": (128, F32),
+    "GO": (128, BF), "WG": (128, BF), "WY": (128, F32), "G15": (128, BF), "DMO": (128, F32), "DME": (128, F32),
+    "C16": (128, F32), "DG": (128, F32), "CW": (128, BF), "G8": (24, BF), "KC": (128, BF), "TH": (128, F32),
+    "CR": (128, F32), "K16": (256, BF), "IOT": (128, BF), "THR": (16, F32), "DUM": (32, F32), "M16": (16, F32),
+    "ZER": (256, BF), "CX": (128, BF), "HY": (16, F32), "OT": (256, BF), "KI": (256, F32), "GI": (128, F32), "ONE": (128, BF),
+    "R32": (256, I32), "RN": (256, I32), "NL": (256, U16), "EV": (256, F32), "ETS": (256, F32), "ST": (256, BF),
+    "AL": (256, U16), "PAY": (256, F16), "VT": (256, BF), "SS": (320, F32), "MB": (256, F32), "WT": (256, BF),
+    "HUB": (256, F16), "MI": (256, F32), "MJ": (256, F32), "NFS": (256, BF),
+    "AI": (2, I32), "UH": (256, BF), "SQ": (256, F32), "QI": (256, I32), "QJ": (256, I32),
+    "FFB": (256, F32), "FF16": (256, F16), "NF32": (32, F32), "DV": (32, F32), "HT": (16, F32), "LK": (32, I32),
+    "LW": (384, BF), "TT": (512, BF), "G": (512, BF), "NS": (16, F32), "TS": (32, F32), "OS": (32, F32), "SL": (32, U16),
+    "GF": (512, F32), "PQ": (512, F32), "XN": (256, BF), "YN": (512, F32), "YP": (256, F32),
+}
+for _t in range(HOPS):
+    for _s in ("r", "s"):
+        SB["%sVL%d" % (_s, _t)] = (32, U16)
+        SB["%sZT%d" % (_s, _t)] = (768, BF)
+        SB["%sOM%d" % (_s, _t)] = (768, BF)
+        SB["%sF%d" % (_s, _t)] = (256, F32)
+del SB["sF3"]
+SCRATCH = {k: ("sbuf", [128, v[0]], v[1]) for k, v in SB.items()}
+for _b in range(8):
+    SCRATCH["P%d" % _b] = ("psum", [128, 512], F32)
+SEMAPHORES = ["v", "s", "p", "gq", "sent"] + ["d%d" % i for i in range(11)] + ["a%d" % i for i in range(15)]
+
+CY, PE, LAT, GA, SC = 1.0, 0.5, 90.0, 1.56, 3.5
+SEARCH, ROUNDS = 1500, 4
+FDVE, RDVE = (1,), ()
+
+
+def R(n, a=0, b=None, st=1, p0=0, p1=128):
+    if n in ("NFC", "ACOL"):
+        a = 36 if n == "NFC" else 37
+        return ("COL", a, a + 1, 1, 0, 128)
+    if b is None:
+        b = SB[n][0] if n in SB else 512
+    return (n, a, b, st, p0, p1)
+
+
+def plan(T, g, topo, core, rank):
+    ops = []
+    nx = T.cores[(rank + STEP) % len(T.cores)]
+    rid, pid, _ = topo.addr(nx)
+    mask = 0
+    for e in topo.engines(core, nx)[::2]:
+        mask |= 1 << e
+    nen = len(topo.engines(core, nx)[::2])
+
+    def ap(r):
+        if isinstance(r, (int, float)) or r is None:
+            return r
+        if r[0] == "ind":
+            return ap(r[1]).indirect(ap(r[2]))
+        return T[r[0]][r[4]:r[5], r[1]:r[2]:r[3]] if r[3] > 1 else T[r[0]][r[4]:r[5], r[1]:r[2]]
+
+    def flat(rs):
+        o = []
+        for r in rs:
+            if isinstance(r, tuple):
+                o += [r[1], r[2]] if r[0] == "ind" else [r]
+        return o
+
+    def ne(r):
+        return 16 * ne(r[2]) if r[0] == "ind" else (r[2] - r[1] + r[3] - 1) // r[3]
+
+    def two(rs):
+        return all(r[0] in SB and SB[r[0]][1] in (BF, F16, U16) for r in rs)
+
+    def add(q, fn, out, ins, cost, sem=None, inc=1, busy=None):
+        w = []
+        rd = flat(ins)
+        for o in out:
+            if o[0] == "ind":
+                w.append(o[1]); rd.append(o[2])
+            else:
+                w.append(o)
+        ops.append({"q": q, "fn": fn, "w": w, "r": rd, "c": cost, "sem": sem or q, "inc": inc,
+                    "busy": cost if busy is None else busy})
+        return len(ops) - 1
+
+    def vc(out, a, full, k):
+        if out[0] == "ind":
+            return 50 + SC * ne(out) * CY
+        if a[0] == "ind":
+            return 50 + GA * ne(a) * CY
+        return 20 + max(64, ne(out) * (k if k else (0.5 if two(full) else 1))) * CY
+    V, S, P = g.vector, g.scalar, g.tensor
+
+    def cp(o, a):
+        add("v", lambda: V.tensor_copy(ap(o), ap(a)), [o], [a], vc(o, a, [o, a], 0))
+
+    def tt(o, a, b, op):
+        add("v", lambda: V.tensor_tensor(ap(o), ap(a), ap(b), op), [o], [a, b],
+            vc(o, a, [], 2 if (a[0] in SB and b[0] in SB) else 1))
+
+    def ts(o, a, s1, op0, s2=None, op1=None):
+        if op1 is None:
+            f = lambda: V.tensor_scalar(ap(o), ap(a), ap(s1), None, op0)
+        else:
+            f = lambda: V.tensor_scalar(ap(o), ap(a), ap(s1), ap(s2), op0, op1)
+        add("v", f, [o], [a, s1, s2], vc(o, a, [o, a], 0))
+
+    def ms(o, c):
+        add("v", lambda: V.memset(ap(o), c), [o], [], vc(o, o, [o], 0))
+
+    def scan(o, a, b, init, op0, op1):
+        add("v", lambda: V.tensor_tensor_scan(ap(o), ap(a), ap(b), init, op0, op1), [o], [a, b], vc(o, a, [], 1))
+
+    def act(o, a, f=AF.Identity, bias=0.0, scale=1.0, acc=None):
+        c = 65 + GA * ne(a) * CY if a[0] == "ind" else 30 + max(64, ne(a)) * CY
+        if acc is None:
+            fn = lambda: S.activation(ap(o), ap(a), f, bias=ap(bias), scale=ap(scale))
+        else:
+            fn = lambda: S.activation(ap(o), ap(a), f, bias=ap(bias), scale=ap(scale), accum_out=ap(acc))
+        add("s", fn, [o] + ([acc] if acc else []), [a, bias, scale], c + (1300 if f == AF.Exp else 0))
+
+    def mm(o, l, r, start=True, stop=True):
+        c = max(min(64, ne(l)), ne(r)) * PE * (4 if SB[l[0]][1] == F32 else 1)
+        add("p", lambda: P.matmul(ap(o), ap(l), ap(r), start, stop), [o], [l, r], c)
+
+    def iota(o, pat, base, cm):
+        if SB[o[0]][1] == I32:
+            f = lambda: g.iota(ap(o), pat, base, cm)
+        else:
+            f = lambda: g.iota(ap(o), pat, base, cm, allow_small_or_imprecise_dtypes=True)
+        add("gq", f, [o], [], 130 + 2 * ne(o) * CY)
+    nd = [0]
+
+    def dma(o, a, out, ins, cost):
+        s = "d%d" % nd[0]
+        nd[0] += 1
+        add("y", lambda: g.sync.dma_start(o(), a()), out, ins, cost, sem=s, inc=16, busy=60)
+        if 1 < nd[0] <= 8:
+            ops[-1]["seq"] = len(ops) - 2
+    na = [0]
+
+    def send(src, dst, cost):
+        s = "a%d" % na[0]
+        na[0] += 1
+        i = add("gq", lambda: g.remote_dma(ap(dst), ap(src), T.sem[s], T.sem.sent, pid, rid, mask), [], [src], cost,
+                sem="sent", inc=0, busy=300)
+        ops.append({"q": None, "w": [dst], "r": [], "c": 0, "sem": s, "inc": nen, "busy": 0, "after": i})
+
+    def ind(w, o):
+        return ("ind", w, o)
+
+    def col(j):
+        return R("COL", j, j + 1)
+
+    def bl(n, b, off=0, w=128):
+        return R(n, off + w * b, off + w * b + w)
+    dma(lambda: T.V0[:], lambda: T.v0[:], [R("V0")], [], 2000)
+    for c in range(4):
+        dma(lambda c=c: T.ENI[:, 512 * c:512 * c + 512], lambda c=c: T.en[:, 512 * c:512 * c + 512],
+            [bl("ENI", c, 0, 512)], [], 2800 + 900 * c)
+    dma(lambda: T.rZT0[:, 256:512], lambda: T.z0[:], [R("rZT0", 256, 512)], [], 5800)
+    dma(lambda: T.WTI[:], lambda: T.wt[:], [R("WTI")], [], 5900)
+    dma(lambda: T.X[:], lambda: T.xs[:], [R("X")], [], 7500)
+    TH0 = 786433.0 - 7
+    iota(R("PI", 0, 1), [[1, 1]], 0, 1)
+    iota(R("KI"), [[0, 16], [1, 16]], 0, 0)
+    iota(R("GI"), [[1, 8], [0, 16]], 0, 0)
+    iota(R("Q1"), [[1, 128]], 0, -1)
+    iota(R("Q3"), [[0, 16], [1, 8]], 0, 0)
+    iota(R("IOT"), [[1, 128]], 0, 0)
+    iota(R("Q0"), [[1, 32], [0, 16]], 0, 0)
+    iota(R("Q2"), [[1, 16], [16, 8]], 0, -1)
+    iota(R("DUM"), [[1, 32]], 2048, 0)
+    iota(R("THR"), [[0, 2], [16, 8]], 0, 0)
+    iota(R("L"), [[0, 2048]], 0, 0)
+    cp(col(0), R("PI", 0, 1))
+    ts(R("PI", 1, 2), R("PI", 0, 1), 15, A.bitwise_and); cp(col(1), R("PI", 1, 2))
+    ts(R("PI", 2, 3), R("PI", 0, 1), 4, A.arith_shift_right); cp(col(2), R("PI", 2, 3))
+    ts(R("PI", 3, 4), R("PI", 0, 1), 1, A.bitwise_and); cp(col(14), R("PI", 3, 4))
+    ts(col(6), col(1), 15.0, A.is_equal)
+    tt(col(4), col(14), col(6), A.subtract)
+    ts(R("PI", 3, 4), R("PI", 0, 1), 31, A.bitwise_and); cp(col(15), R("PI", 3, 4))
+    ts(col(16), col(15), 16.0, A.is_ge, 128.0, A.mult)
+    for j, c in ((30, 1.0), (19, 1e29), (20, 100 * math.log(2.0)), (21, 100 * math.log(2.0) + math.log(3.5)),
+                 (22, 129 - 1023.5 / 2048), (23, 592.0 + 264192), (24, -2048.0), (28, 1.5 * 2.0 ** 27), (29, 7 * 2048.0),
+                 (31, -63.5), (32, 8 * 2.0 ** 20 + TH0), (33, 32768.0),
+                 (35, 1 - 8 * 2.0 ** 20 - TH0)):
+        ms(col(j), c)
+    act(col(5), col(14), bias=col(30), scale=-1.0)
+    for t in range(HOPS):
+        act(col(10 + t), col(6), scale=2048.0 * (9 + t))
+    act(col(17), col(1), bias=col(30))
+    act(col(18), col(1), scale=32.0)
+    act(col(8), col(19), scale=1e4)
+    act(col(27), col(2), bias=col(35), scale=2.0 ** 20)
+    ts(R("M16"), R("KI", 0, 16), col(1), A.is_equal)
+    ts(R("I3"), R("Q1"), 0.0, A.is_equal)
+    for n, c in (("I", 1.0), ("NI", -1.0), ("N2I", -2048.0), ("BI", 512.0), ("DMO", col(4)), ("DME", col(5))):
+        act(R(n), R("I3"), scale=c)
+    ts(R("EXP"), R("Q0"), col(15), A.is_equal)
+    ts(R("GO"), R("GI"), col(2), A.is_equal)
+    act(R("WY"), R("GO"), scale=col(17))
+    cp(col(3), R("WTI"))
+    act(R("WG"), R("GO"), scale=col(3))
+    ts(R("Q3"), R("Q3"), col(2), A.is_equal)
+    for j, c in enumerate((512.0, -256.0)):
+        act(R("G8", 8 * j + 8, 8 * j + 16), R("Q3", 0, 8), scale=c)
+    act(R("G15"), R("GO"), scale=0.0); act(R("G15", 15, 128, 16), R("Q3", 0, 8))
+    ms(R("ONE"), 1.0); ms(R("ZER"), 0.0); ms(R("SS", 128, 160), 0.0); ms(R("SS", 288, 320), 0.0)
+    act(R("C16"), R("ONE"), scale=1.0 / 16)
+    for j in range(8):
+        act(R("L", 16 * j, 16 * j + 129 * 15 + 1, 129), R("ONE", 0, 16), scale=R("Q3", j, j + 1))
+    ts(R("DG"), R("Q2"), 0.0, A.is_equal)
+    act(R("Q2"), R("DG"), scale=4096.0 - 2.0 ** 20)
+    act(R("Q1"), R("Q3"), scale=-4096.0)
+    tt(R("CW"), R("Q2"), R("Q1"), A.add)
+    act(R("TH"), R("GI"), bias=col(32), scale=-2.0 ** 20)
+    for j, p, c in ((38, 0, -2.0 ** 20), (39, 1, 16.0), (40, 2, -4096.0), (41, 3, -135.0)):
+        ts(col(j), col(0), float(p), A.is_equal, c, A.mult)
+    act(col(34), col(38), bias=col(40), scale=-9.0); act(col(34), col(34), bias=col(41))
+    act(R("Q4"), R("KI", 0, 128), bias=col(34), scale=col(39))
+    act(R("GI"), R("GI"), scale=col(38))
+    tt(R("KC"), R("Q4"), R("GI"), A.add)
+    ts(R("CR"), R("KI", 0, 128), 1.0, A.min, 2e9, A.mult)
+    act(R("K16"), R("KI"), bias=col(33), scale=-2048.0)
+    act(R("DUM"), R("DUM"), bias=col(18))
+    act(R("THR"), R("THR"), bias=col(1))
+    act(col(7), col(0), AF.Exp, bias=col(20), scale=-math.log(3.0))
+    act(R("THR"), R("THR"), AF.Exp, bias=col(21), scale=-math.log(3.0))
+    ops[-1]["c"] = ops[-1]["busy"] = 100
+    ts(col(25), col(0), 0.0, A.is_equal, -128.0, A.mult); ts(col(26), col(0), 1.0, A.is_equal, -63.5, A.mult)
+    ts(R("CX"), R("KI", 0, 128), col(25), A.mult, col(26), A.add)
+    act(R("IOT"), R("IOT"), bias=col(31))
+    ms(R("ACOL"), -350464.0)
+    for c in range(4):
+        cp(bl("E", c, 0, 512), bl("ENI", c, 0, 512))
+    D, K, FM = ("P3", "P4"), ("P5", "P6"), "P7"
+    MAG = 1.5 * 2.0 ** 30
+
+    def table(OM, b, ff):
+        x = R(K[b], 128, 256)
+        mm(x, R("ONE"), R("CX"), True, False)
+        if ff:
+            mm(x, bl("FF16", b), R("GO"), False, False)
+        mm(x, bl("HUB", b), R("GO"), False, True)
+        x0 = R(K[b], 128, 256, 16)
+        ts(bl("HY", b, 0, 8), x0, MAG, A.add, -MAG, A.add)
+        ts(bl("OT", b), x, MAG, A.add, MAG, A.is_equal)
+        tt(bl("HT", b, 0, 8), x0, bl("HY", b, 0, 8), A.subtract)
+        act(bl("LW", b), bl("OT", b), scale=col(7))
+        if b == 0:
+            act(R("LW", 256, 384), bl("OT", 0), scale=col(8))
+            mm(R(FM, 0, 256), R("I"), R("ZER"), True, False)
+        for a in range(4):
+            for c in (8 * b + 2 * a, 8 * b + 2 * a + 1):
+                ts(bl("RH", c), R("IOT"), R("HT", c, c + 1), A.is_equal)
+            r = R("RH", 1024 * b + 256 * a, 1024 * b + 256 * a + 256)
+            o1 = R(FM, 0, 256, 1, 32 * a, 32 * a + 32)
+            if b == 0:
+                mm(R(K[0], 256, 512, 1, 32 * a, 32 * a + 32), R("LW", 32 * a, 32 * a + 32), r)
+                mm(o1, R("LW", 256 + 32 * a, 288 + 32 * a), r, False, False)
+            else:
+                mm(o1, R("LW", 128 + 32 * a, 160 + 32 * a), r, False, True)
+        mm(R(D[b], 384, 512), bl("OT", b), R("I"))
+        act(bl(OM, b), R(D[b], 384, 512))
+        return R(K[0], 256, 512) if b == 0 else R(FM, 0, 256)
+
+    def look(VL, src):
+        cp(R("LK", 0, 16), src)
+        ts(R("LK", 16, 32), R("LK", 0, 16), 127, A.bitwise_and)
+        for b in range(2):
+            ts(bl(VL, b, 16, 8), bl("LK", b, 16, 8), col(16), A.add, 256.0 * b, A.add)
+    cp(R("rVL0", 0, 16), R("V0")); cp(R("NF32", 16, 32), R("V0"))
+    for l in range(16):
+        ts(R("HUB", l, 256, 16), R("NF32", 16, 32), R("M16", l, l + 1), A.mult)
+    look("rVL0", R("V0"))
+    for b in range(2):
+        act(bl("rOM0", b, 256, 256), table("rOM0", b, False))
+    mm(R("P1", 0, 256), R("G15"), R("HUB")); act(R("rF0"), R("P1", 0, 256))
+    for b in range(2):
+        mm(bl("P2", b), bl("rZT0", b, 256), R("I"))
+    act(R("rZT0", 512, 768), R("P2", 0, 256))
+    rot = [0]
+
+    def spread(src, off, c):
+        bk = "P%d" % (rot[0] % 3)
+        rot[0] += 1
+        b, q = divmod(c, 4)
+        mm(R(bk), R(src, off + 128 * b, off + 128 * b + 128, 1, 32 * q, 32 * q + 32), R("EXP", 0, 512, 1, 32 * q, 32 * q + 32))
+        return R(bk)
+    prev = {}
+
+    def chain(key):
+        key = (key, ops[-1]["q"])
+        if key in prev:
+            ops[-1]["seq"] = prev[key]
+        prev[key] = len(ops) - 1
+
+    def gather(o, w, l, dve):
+        if dve:
+            cp(o, ind(w, l))
+        else:
+            act(o, ind(w, l))
+        chain("g")
+    EW = R("E", 0, 2048)
+    for t in range(HOPS):
+        last = t == HOPS - 1
+        VL, ZT, OM, FV = "rVL%d" % t, "rZT%d" % t, "rOM%d" % t, "rF%d" % t
+        sVL, sZT, sOM, sF = "sVL%d" % t, "sZT%d" % t, "sOM%d" % t, "sF%d" % t
+        n = t + 1
+        Z = R(ZT, 256, 512)
+        mm(R(FM, 0, 256), R("WG"), Z)
+        act(R("UH"), R(FM, 0, 256), bias=col(22), scale=1.0 / 2048)
+        mm(R(FM, 256, 512), R("WG"), Z, True, False); mm(R(FM, 256, 512), R("N2I"), R("UH"), False, True)
+        act(R("SQ"), R(FM, 256, 512), AF.Square, bias=col(23))
+        ts(R("QI"), R("SQ"), R("ACOL"), A.add)
+        ts(R("QJ"), R("QI"), 5, A.arith_shift_right, 2047, A.bitwise_and)
+        ts(R("FFB"), R("QJ"), -264192.0, A.add); ts(R("FF16"), R("QJ"), 1.0 / 16, A.mult)
+        if t:
+            mm(R(FM, 0, 256), R("I"), R(ZT, 0, 256), True, False); mm(R(FM, 0, 256), R("NI"), R("K16"), False, True)
+            act(R("VT"), R(FM, 0, 256), AF.Relu)
+        cp(R("NF32", 0, 16), R(VL, 0, 16))
+        for b in range(2):
+            cp(bl("R32", b), ind(EW if t else R("ENI"), bl(VL, b, 0, 8)))
+            ts(bl("RN", b), bl("R32", b), 2047, A.bitwise_and)
+            cp(bl("NL", b), bl("RN", b))
+        act(R("EV"), ind(EW, R(VL, 0, 16)))
+        mm(R(D[1], 0, 256), R("DME"), R("EV"), True, False); mm(R(D[1], 0, 256), R("I3"), R(FV), False, True)
+        act(R("PQ", 256, 512), R(D[1], 0, 256), bias=col(10 + t))
+        if last:
+            for c in range(4):
+                mm(R(K[c % 2]), R("WY"), bl("E", c, 0, 512))
+                act(bl("YT", c, 0, 512), R(K[c % 2]))
+        for c in range(8):
+            gather(bl("F", c, 0, 512), EW, bl("NL", c, 0, 32), c in FDVE)
+        for b in range(2):
+            for k in range(16):
+                j = (k + t) % 16
+                mm(R(D[b], k, 128, 16), R("F", 2048 * b + k, 2048 * b + 2048, 16), R("DG", 8 * j, 8 * j + 8))
+            cp(bl("ETS", b), R(D[b], 0, 128))
+            ts(bl("ST", b), R(D[b], 0, 128), 1.0 / 2048, A.mult, 129 - 1023.5 / 2048, A.add)
+            mm(R(D[b], 128, 256), bl("ETS", b), R("I3"), True, False)
+            mm(R(D[b], 128, 256), bl("ST", b), R("N2I"), False, True)
+            ts(bl("AL", b), R(D[b], 128, 256), 264192.0, A.add)
+            for c in range(4 * b, 4 * b + 4):
+                if t == 0:
+                    ts(bl("CM", c, 0, 512), bl("F", c, 0, 512), 2048.0, A.is_ge)
+                else:
+                    tt(bl("CM", c, 0, 512), bl("F", c, 0, 512), spread(ZT, 0, c), A.is_ge)
+                chain("c")
+        for c in range(8):
+            gather(bl("RW", c, 0, 512), R("X"), bl("AL", c, 0, 32), c in RDVE)
+            tt(bl("MX", c, 0, 512), bl("RW", c, 0, 512), spread(ZT, 512, c), A.max)
+            chain("c")
+        for b in range(2):
+            tt(bl("PAY", b), R(D[b], 128, 256), bl("FFB", b), A.subtract)
+            kb = R(K[b], 0, 128)
+            mm(kb, R("ONE"), R("KC"), True, False)
+            if t:
+                mm(kb, R("BI"), bl("VT", b), False, False)
+            for src in ("CM", "ST", "RW", "MX"):
+                if src == "ST":
+                    mm(kb, R("I"), bl("ST", b), False, False)
+                    continue
+                for k in range(16):
+                    j = (k + t) % 16
+                    w = R("CW", 8 * j, 8 * j + 8) if src == "CM" else R("G8", 16, 24) if src == "RW" else R("G8", 8, 16)
+                    mm(R(K[b], k, 128, 16), R(src, 2048 * b + k, 2048 * b + 2048, 16), w, False, src == "MX" and k == 15)
+            s0 = 160 * b
+            scan(R("SS", s0, s0 + 128), R("TH"), kb, 1e9, A.min, A.min)
+            scan(bl("MB", b), R("CR"), R("SS", s0 + 15, s0 + 143), 0.0, A.min, A.max)
+            tt(bl("WT", b), kb, bl("MB", b), A.is_equal)
+            mm(R(D[b], 256, 384), bl("WT", b), R("I"))
+            tt(bl("HUB", b), R(D[b], 256, 384), bl("PAY", b), A.mult)
+            tb = table(sOM, b, True)
+            tt(bl("TT", b, 0, 256), tb, bl(OM, b, 256, 256), A.add)
+            if not last:
+                act(bl(sOM, b, 256, 256), tb)
+        for src in ("FF16", "HUB"):
+            for l in range(16):
+                mm(R("P0", 0, 16), R("L", 128 * l, 128 * l + 128), R(src, l, 256, 16), src == "FF16" and l == 0, src == "HUB" and l == 15)
+        FL = R(sVL, 0, 16)
+        cp(FL, R("P0", 0, 16))
+        look(sVL, R("P0", 0, 16))
+        cp(R("NF32", 16, 32), FL)
+        tt(R("G", 0, 256), ind(R("TT"), R(VL, 16, 32)), R(OM, 0, 256), A.mult)
+        tt(R("G", 256, 512), ind(R("TT"), R(sVL, 16, 32)), R(sOM, 0, 256), A.mult)
+        for h in range(2):
+            for l in range(16):
+                mm(R(D[1], 0, 16), R("L", 128 * l, 128 * l + 128), R("G", 256 * h + l, 256 * h + 256, 16),
+                   h == 0 and l == 0, h == 1 and l == 15)
+        tt(R("DV"), R("DUM"), R("NF32"), A.subtract)
+        tt(R("NS"), R(D[1], 0, 16), R("THR"), A.is_ge)
+        for h in range(2):
+            tt(bl("TS", h, 0, 16), R("NS"), bl("DV", h, 0, 16), A.mult)
+        tt(R("OS"), R("TS"), R("NF32"), A.add)
+        cp(R("SL"), R("OS"))
+        act(R("GF", 0, 256), ind(EW, FL), scale=col(5))
+        act(R("GF", 256, 512), ind(EW, FL), scale=col(4))
+        mm(R("P2", 0, 256), R("DMO"), R("EV"), True, False); mm(R("P2", 0, 256), R("G15"), R("FF16"), False, False)
+        mm(R("P2", 0, 256), R("G15"), R("HUB"), False, True)
+        act(R("PQ", 0, 256), R("P2", 0, 256), bias=col(10 + t))
+        act(R("MI"), R("MB"), bias=col(28))
+        act(R("MJ"), R("MI"), bias=col(28), scale=-1.0)
+        mm(R(K[1], 256, 512), R("I3"), R("MB"), True, False); mm(R(K[1], 256, 512), R("I3"), R("MJ"), False, True)
+        act(R(sZT, 0, 256), R(K[1], 256, 512), bias=col(29), scale=2048.0)
+        for b in range(2):
+            mm(bl("P1", b), bl("MB", b), R("I3"))
+        act(R("NFS"), R("P1", 0, 256), AF.Relu, bias=col(27), acc=None if last else R("NFC"))
+        tt(R("XN"), ind(R("X"), FL), R("NFS"), A.mult)
+        o1 = R("P1", 0, 256)
+        mm(o1, R("G15"), R("FF16"), True, False); mm(o1, R("G15"), R("HUB"), False, not last)
+        if last:
+            for b in range(2):
+                mm(bl("P1", b), bl(sZT, b), R("I"), False, b == 1)
+            act(R("YP"), o1, bias=col(24))
+            dma(lambda: T.yp[:], lambda: T.YP[15:128:16, :], [], [R("YP")], 2200)
+        else:
+            act(R(sF), o1)
+        mm(o1, R("I"), Z, True, False); mm(o1, R("NI"), R("XN"), False, True)
+        if last:
+            act(R(sZT, 256, 512), o1, AF.Abs)
+            dma(lambda s=sZT: T.yz[:], lambda s=sZT: T[s][:, 256:512], [], [R(sZT, 256, 512)], 2200)
+            mm(R("P2"), R("WY"), R("GF"), True, False); mm(R("P2"), R("WY"), R("PQ"), False, True)
+            act(R("YN"), R("P2"))
+            cp(ind(R("YT"), R("SL")), R("YN"))
+            dma(lambda: T.ys[:], lambda: T.YT[0:128:16, 0:2048], [], [R("YT")], 2200)
+        else:
+            for b in range(2):
+                o = bl("P1", b, 256)
+                mm(o, bl(ZT, b, 256), R("I"), True, False); mm(o, bl("XN", b), R("NI"), False, True)
+            act(R(sZT, 256, 768), R("P1"), AF.Abs)
+            mm(R("P2", 0, 1), R("C16"), R("NFC"))
+            cp(R("AI", 0, 1), R("P2", 0, 1))
+            ts(R("AI", 1, 2), R("AI", 0, 1), 255, A.bitwise_and)
+            ts(R("ACOL"), R("AI", 1, 2), 32.0, A.mult, -350464.0, A.add)
+            send(R(sVL), R("rVL%d" % n), 2200)
+            send(R(sZT, 0, 256), R("rZT%d" % n, 0, 256), 2600)
+            send(R(sZT, 256, 768), R("rZT%d" % n, 256, 768), 3100)
+            send(R(sF), R("rF%d" % n), 3000)
+            send(R(sOM), R("rOM%d" % n), 3500)
+            tt(ind(R("E"), R("SL")), R("GF"), R("PQ"), A.add)
+    return ops, nen * na[0]
+
+
+def schedule(ops):
+    hist = {}
+    for i, o in enumerate(ops):
+        dep = set()
+        if "after" in o:
+            dep.add(o["after"])
+        for rs, wr in ((o["r"], False), (o["w"], True)):
+            for r in rs:
+                ps = r[0] not in SB
+                a, b, st = (0, 512, 1) if ps else (r[1], r[2], r[3])
+                x = wr or ps
+                h = hist.setdefault(r[0], [])
+                for (j, c, d, y, s2) in h:
+                    if j != i and c < b and a < d and (x or y) and not (st == s2 and (a - c) % st):
+                        dep.add(j)
+                if x and st == 1:
+                    h[:] = [e for e in h if not (a <= e[1] and e[2] <= b)]
+                h.append((i, a, b, x, st))
+        o["dep"] = dep
+    n = len(ops)
+    suc = [[] for _ in range(n)]
+    for i, o in enumerate(ops):
+        o["all"] = set(o["dep"]) | ({o["seq"]} if "seq" in o else set())
+        for j in o["all"]:
+            suc[j].append(i)
+
+    def lat(j, i):
+        if j not in ops[i]["dep"]:
+            return ops[j]["busy"] - ops[j]["c"]
+        return 0.0 if ops[j]["q"] == "p" and ops[i]["q"] == "p" else LAT
+
+    def place(keyf, pred, succ, back):
+        left = [len(pred[i]) for i in range(n)]
+        heap = sorted((keyf[i], i) for i in range(n) if left[i] == 0)
+        st = [0.0] * n
+        rdy = [0.0] * n
+        slots = {}
+        while heap:
+            _, i = heap.pop(0)
+            o = ops[i]
+            s = rdy[i]
+            if o["q"]:
+                sl = slots.setdefault(o["q"], [])
+                off = o["c"] - o["busy"] if back else 0.0
+                s += off
+                k = len(sl)
+                while k > 0 and sl[k - 1][1] > s:
+                    k -= 1
+                while k < len(sl) and sl[k][0] < s + o["busy"]:
+                    s = max(s, sl[k][1])
+                    k += 1
+                sl.insert(k, (s, s + o["busy"]))
+                s -= off
+            st[i] = s
+            for k in succ[i]:
+                e = s + o["c"] + (lat(k, i) if back else lat(i, k))
+                if e > rdy[k]:
+                    rdy[k] = e
+                left[k] -= 1
+                if left[k] == 0:
+                    lo, hi, x = 0, len(heap), (keyf[k], k)
+                    while lo < hi:
+                        m = (lo + hi) // 2
+                        if heap[m] < x:
+                            lo = m + 1
+                        else:
+                            hi = m
+                    heap.insert(lo, x)
+        return st
+    pred = [sorted(o["all"]) for o in ops]
+    pr = [0.0] * n
+    for i in range(n - 1, -1, -1):
+        pr[i] = ops[i]["c"] + max([pr[k] + lat(i, k) for k in suc[i]] + [0.0])
+    best = None
+    for it in range(2 * ROUNDS):
+        if it % ROUNDS == 0:
+            key = [-x for x in pr] if it else [float(i) for i in range(n)]
+        st = place(key, pred, suc, False)
+        end = max(st[i] + ops[i]["c"] for i in range(n))
+        if best is None or end < best[0]:
+            best = (end, st)
+        bk = place([-(st[i] + ops[i]["c"]) for i in range(n)], suc, pred, True)
+        key = [-(bk[i] + ops[i]["c"]) for i in range(n)]
+    rs = 12345
+    cur = best
+    for it in range(SEARCH):
+        key = []
+        amp = (200.0, 600.0, 1500.0)[it % 3]
+        for i in range(n):
+            rs = (rs * 1103515245 + 12345) % 2147483648
+            key.append(-(cur[1][i] + ops[i]["c"]) + amp * (rs / 2147483648.0))
+        bk = place(key, suc, pred, True)
+        st = place([-(bk[i] + ops[i]["c"]) for i in range(n)], pred, suc, False)
+        end = max(st[i] + ops[i]["c"] for i in range(n))
+        if end < cur[0] + 300:
+            cur = (end, st)
+        if end < best[0]:
+            best = (end, st)
+    st = best[1]
+    for i in range(n):
+        ops[i]["t"] = (st[i], st[i] + ops[i]["c"])
+    return sorted(range(n), key=lambda i: (st[i], i))
+
+
+ORDER = []
+
+
+def rank_program(g, core, T, topo):
+    rank = T.rank_of(core)
+    if rank is None:
+        return
+    ops, sent = plan(T, g, topo, core, rank)
+    if not ORDER:
+        ORDER.append(schedule(ops))
+        ORDER.append([o["dep"] for o in ops])
+    Q = {"v": g.vector, "s": g.scalar, "p": g.tensor, "gq": g, "y": g.sync}
+    cnt, seen = {}, {}
+    for i in ORDER[0]:
+        o = ops[i]
+        q = o["q"]
+        if q:
+            need = {}
+            for j in ORDER[1][i]:
+                d = ops[j]
+                if (q == "p" and d["q"] == "p") or d["inc"] == 0:
+                    continue
+                need[d["sem"]] = max(need.get(d["sem"], 0), d["val"])
+            for s in sorted(need):
+                if seen.get((q, s), 0) < need[s]:
+                    Q[q].wait_ge(T.sem[s], need[s])
+                    seen[(q, s)] = need[s]
+            ins = o["fn"]()
+            if o["inc"]:
+                ins.then_inc(T.sem[o["sem"]], o["inc"])
+        cnt[o["sem"]] = cnt.get(o["sem"], 0) + o["inc"]
+        o["val"] = cnt[o["sem"]]
+    cnt["sent"] = sent
+    for s in sorted(cnt):
+        g.sync.wait_ge(T.sem[s], cnt[s])

@@ -4,21 +4,21 @@ from concourse.mybir import AluOpType as A, ActivationFunctionType as AF
 HOPS, STEP = 4, 3
 F32, BF, F16, I32, U16 = "float32", "bfloat16", "float16", "int32", "uint16"
 SB = {
-    "ENI": (2048, I32), "E": (2560, F32), "X": (2048, BF), "YT": (2560, F32), "V0": (16, I32), "WTI": (1, I32),
+    "ENI": (2048, I32), "E": (2560, F32), "X": (2048, BF), "YT": (128, F32), "V0": (16, I32), "WTI": (1, I32),
     "F": (4096, F32), "CM": (4096, BF), "RW": (4096, BF), "MX": (4096, BF), "RH": (2048, BF),
-    "L": (2048, BF), "EXP": (512, BF), "Q0": (512, BF), "Q1": (128, F32), "Q2": (128, F32), "Q3": (128, F32), "Q4": (128, F32),
+    "L": (2048, BF), "EXP": (512, BF), "Q0": (512, BF), "Q1": (128, F32), "Q2": (128, F32), "Q3": (128, F32),
     "PI": (4, I32), "COL": (42, F32), "I": (128, BF), "NI": (128, BF), "N2I": (128, BF), "BI": (128, BF), "I3": (128, F32),
-    "GO": (128, BF), "WG": (128, BF), "WY": (128, F32), "G15": (128, BF), "DMO": (128, F32), "DME": (128, F32),
+    "GO": (128, BF), "WG": (128, BF), "WY": (8, F32), "G15": (128, BF), "DMO": (128, F32), "DME": (128, F32),
     "C16": (128, F32), "DG": (128, F32), "CW": (128, BF), "G8": (24, BF), "KC": (128, BF), "TH": (128, F32),
-    "CR": (128, F32), "K16": (256, BF), "IOT": (128, BF), "THR": (16, F32), "DUM": (32, F32), "M16": (16, F32),
+    "CR": (128, F32), "K16": (256, BF), "IOT": (128, BF), "THR": (16, F32), "DUM": (32, F32),
     "ZER": (256, BF), "CX": (128, BF), "HY": (16, F32), "OT": (256, BF), "KI": (256, F32), "GI": (128, F32), "ONE": (128, BF),
     "R32": (256, I32), "RN": (256, I32), "NL": (256, U16), "EV": (256, F32), "ETS": (256, F32), "ST": (256, BF),
     "AL": (256, U16), "PAY": (256, F16), "VT": (256, BF), "SS": (320, F32), "MB": (256, F32), "WT": (256, BF),
-    "HUB": (256, F16), "MI": (256, F32), "MJ": (256, F32), "NFS": (256, BF),
+    "HUB": (256, F16), "SG": (256, BF), "HS": (256, BF), "NG": (128, BF), "NFS": (256, BF),
     "AI": (2, I32), "UH": (256, BF), "SQ": (256, F32), "QI": (256, I32), "QJ": (256, I32),
     "FFB": (256, F32), "FF16": (256, F16), "NF32": (32, F32), "DV": (32, F32), "HT": (16, F32), "LK": (32, I32),
     "LW": (384, BF), "TT": (512, BF), "G": (512, BF), "NS": (16, F32), "TS": (32, F32), "OS": (32, F32), "SL": (32, U16),
-    "GF": (512, F32), "PQ": (512, F32), "XN": (256, BF), "YN": (512, F32), "YP": (256, F32),
+    "GF": (512, F32), "PQ": (512, F32), "XN": (256, BF), "XR": (256, BF), "YN": (128, F32), "YP": (256, F32),
 }
 for _t in range(HOPS):
     for _s in ("r", "s"):
@@ -32,9 +32,13 @@ for _b in range(8):
     SCRATCH["P%d" % _b] = ("psum", [128, 512], F32)
 SEMAPHORES = ["v", "s", "p", "gq", "sent"] + ["d%d" % i for i in range(11)] + ["a%d" % i for i in range(15)]
 
-CY, PE, LAT, GA, SC = 1.0, 0.5, 90.0, 1.56, 3.5
-SEARCH, ROUNDS = 1500, 4
-FDVE, RDVE = (1,), ()
+CY, PE, LAT, GA, SC = 1.0, 0.5, 140.0, 1.56, 3.5
+COM, GROUPS = 2000, 500
+SEARCH, ROUNDS = 300, 4
+FDVE, RDVE = (2, 3), ()
+TH0 = 655360.0 - 6
+NUM = {30: 1.0, 20: 100 * math.log(2.0), 21: 100 * math.log(2.0) + math.log(3.5), 22: 129 - 1023.5 / 2048, 23: 592.0 + 264192,
+       24: -2048.0, 31: -63.5, 32: 8 * 2.0 ** 20 + TH0, 33: 32768.0}
 
 
 def R(n, a=0, b=None, st=1, p0=0, p1=128):
@@ -144,6 +148,7 @@ def plan(T, g, topo, core, rank):
     na = [0]
 
     def send(src, dst, cost):
+        cost += COM
         s = "a%d" % na[0]
         na[0] += 1
         i = add("gq", lambda: g.remote_dma(ap(dst), ap(src), T.sem[s], T.sem.sent, pid, rid, mask), [], [src], cost,
@@ -154,6 +159,8 @@ def plan(T, g, topo, core, rank):
         return ("ind", w, o)
 
     def col(j):
+        if j in NUM:
+            return NUM[j]
         return R("COL", j, j + 1)
 
     def bl(n, b, off=0, w=128):
@@ -165,7 +172,6 @@ def plan(T, g, topo, core, rank):
     dma(lambda: T.rZT0[:, 256:512], lambda: T.z0[:], [R("rZT0", 256, 512)], [], 5800)
     dma(lambda: T.WTI[:], lambda: T.wt[:], [R("WTI")], [], 5900)
     dma(lambda: T.X[:], lambda: T.xs[:], [R("X")], [], 7500)
-    TH0 = 786433.0 - 7
     iota(R("PI", 0, 1), [[1, 1]], 0, 1)
     iota(R("KI"), [[0, 16], [1, 16]], 0, 0)
     iota(R("GI"), [[1, 8], [0, 16]], 0, 0)
@@ -185,28 +191,24 @@ def plan(T, g, topo, core, rank):
     tt(col(4), col(14), col(6), A.subtract)
     ts(R("PI", 3, 4), R("PI", 0, 1), 31, A.bitwise_and); cp(col(15), R("PI", 3, 4))
     ts(col(16), col(15), 16.0, A.is_ge, 128.0, A.mult)
-    for j, c in ((30, 1.0), (19, 1e29), (20, 100 * math.log(2.0)), (21, 100 * math.log(2.0) + math.log(3.5)),
-                 (22, 129 - 1023.5 / 2048), (23, 592.0 + 264192), (24, -2048.0), (28, 1.5 * 2.0 ** 27), (29, 7 * 2048.0),
-                 (31, -63.5), (32, 8 * 2.0 ** 20 + TH0), (33, 32768.0),
-                 (35, 1 - 8 * 2.0 ** 20 - TH0)):
-        ms(col(j), c)
+    ms(col(19), 1e29)
     act(col(5), col(14), bias=col(30), scale=-1.0)
     for t in range(HOPS):
         act(col(10 + t), col(6), scale=2048.0 * (9 + t))
     act(col(17), col(1), bias=col(30))
     act(col(18), col(1), scale=32.0)
     act(col(8), col(19), scale=1e4)
-    act(col(27), col(2), bias=col(35), scale=2.0 ** 20)
-    ts(R("M16"), R("KI", 0, 16), col(1), A.is_equal)
+    ts(R("WT"), R("KI"), col(1), A.is_equal); cp(R("SL", 0, 16), R("KI", 0, 16))
     ts(R("I3"), R("Q1"), 0.0, A.is_equal)
     for n, c in (("I", 1.0), ("NI", -1.0), ("N2I", -2048.0), ("BI", 512.0), ("DMO", col(4)), ("DME", col(5))):
         act(R(n), R("I3"), scale=c)
     ts(R("EXP"), R("Q0"), col(15), A.is_equal)
     ts(R("GO"), R("GI"), col(2), A.is_equal)
-    act(R("WY"), R("GO"), scale=col(17))
+    act(R("NG"), R("GO"), scale=-64.0)
     cp(col(3), R("WTI"))
     act(R("WG"), R("GO"), scale=col(3))
     ts(R("Q3"), R("Q3"), col(2), A.is_equal)
+    act(R("WY"), R("Q3", 0, 8), scale=col(17))
     for j, c in enumerate((512.0, -256.0)):
         act(R("G8", 8 * j + 8, 8 * j + 16), R("Q3", 0, 8), scale=c)
     act(R("G15"), R("GO"), scale=0.0); act(R("G15", 15, 128, 16), R("Q3", 0, 8))
@@ -222,9 +224,9 @@ def plan(T, g, topo, core, rank):
     for j, p, c in ((38, 0, -2.0 ** 20), (39, 1, 16.0), (40, 2, -4096.0), (41, 3, -135.0)):
         ts(col(j), col(0), float(p), A.is_equal, c, A.mult)
     act(col(34), col(38), bias=col(40), scale=-9.0); act(col(34), col(34), bias=col(41))
-    act(R("Q4"), R("KI", 0, 128), bias=col(34), scale=col(39))
+    act(R("MB", 0, 128), R("KI", 0, 128), bias=col(34), scale=col(39))
     act(R("GI"), R("GI"), scale=col(38))
-    tt(R("KC"), R("Q4"), R("GI"), A.add)
+    tt(R("KC"), R("MB", 0, 128), R("GI"), A.add)
     ts(R("CR"), R("KI", 0, 128), 1.0, A.min, 2e9, A.mult)
     act(R("K16"), R("KI"), bias=col(33), scale=-2048.0)
     act(R("DUM"), R("DUM"), bias=col(18))
@@ -241,7 +243,7 @@ def plan(T, g, topo, core, rank):
     D, K, FM = ("P3", "P4"), ("P5", "P6"), "P7"
     MAG = 1.5 * 2.0 ** 30
 
-    def table(OM, b, ff):
+    def table(OM, b, ff, base=None, pure=True):
         x = R(K[b], 128, 256)
         mm(x, R("ONE"), R("CX"), True, False)
         if ff:
@@ -254,20 +256,28 @@ def plan(T, g, topo, core, rank):
         act(bl("LW", b), bl("OT", b), scale=col(7))
         if b == 0:
             act(R("LW", 256, 384), bl("OT", 0), scale=col(8))
-            mm(R(FM, 0, 256), R("I"), R("ZER"), True, False)
-        for a in range(4):
-            for c in (8 * b + 2 * a, 8 * b + 2 * a + 1):
-                ts(bl("RH", c), R("IOT"), R("HT", c, c + 1), A.is_equal)
-            r = R("RH", 1024 * b + 256 * a, 1024 * b + 256 * a + 256)
-            o1 = R(FM, 0, 256, 1, 32 * a, 32 * a + 32)
-            if b == 0:
-                mm(R(K[0], 256, 512, 1, 32 * a, 32 * a + 32), R("LW", 32 * a, 32 * a + 32), r)
-                mm(o1, R("LW", 256 + 32 * a, 288 + 32 * a), r, False, False)
-            else:
-                mm(o1, R("LW", 128 + 32 * a, 160 + 32 * a), r, False, True)
+        for c in range(8 * b, 8 * b + 8):
+            ts(bl("RH", c), R("IOT"), R("HT", c, c + 1), A.is_equal)
         mm(R(D[b], 384, 512), bl("OT", b), R("I"))
         act(bl(OM, b), R(D[b], 384, 512))
-        return R(K[0], 256, 512) if b == 0 else R(FM, 0, 256)
+
+        def sums(k0, k1, s0, s1, d0, d1):
+            if b == 0:
+                mm(R(k1, 0, 256), R("I"), s1, True, False)
+                mm(R(k0, 256, 512), R("I"), s0, True, False)
+            for a in range(4):
+                r = R("RH", 1024 * b + 256 * a, 1024 * b + 256 * a + 256)
+                o1 = R(k1, 0, 256, 1, 32 * a, 32 * a + 32)
+                if b == 0:
+                    mm(R(k0, 256, 512, 1, 32 * a, 32 * a + 32), R("LW", 32 * a, 32 * a + 32), r, False, True)
+                    mm(o1, R("LW", 256 + 32 * a, 288 + 32 * a), r, False, False)
+                else:
+                    mm(o1, R("LW", 128 + 32 * a, 160 + 32 * a), r, False, True)
+            act(d1 if b else d0, R(k1, 0, 256) if b else R(k0, 256, 512))
+        if base:
+            sums(K[0], FM, R(base, 256, 512), R(base, 512, 768), R("TT", 0, 256), R("TT", 256, 512))
+        if pure:
+            sums(K[0], D[0], R("ZER"), R("ZER"), R(OM, 256, 512), R(OM, 512, 768))
 
     def look(VL, src):
         cp(R("LK", 0, 16), src)
@@ -275,20 +285,17 @@ def plan(T, g, topo, core, rank):
         for b in range(2):
             ts(bl(VL, b, 16, 8), bl("LK", b, 16, 8), col(16), A.add, 256.0 * b, A.add)
     cp(R("rVL0", 0, 16), R("V0")); cp(R("NF32", 16, 32), R("V0"))
-    for l in range(16):
-        ts(R("HUB", l, 256, 16), R("NF32", 16, 32), R("M16", l, l + 1), A.mult)
+    tt(R("HUB"), ind(R("NF32", 16, 32), R("SL", 0, 16)), R("WT"), A.mult)
     look("rVL0", R("V0"))
     for b in range(2):
-        act(bl("rOM0", b, 256, 256), table("rOM0", b, False))
+        table("rOM0", b, False)
     mm(R("P1", 0, 256), R("G15"), R("HUB")); act(R("rF0"), R("P1", 0, 256))
     for b in range(2):
         mm(bl("P2", b), bl("rZT0", b, 256), R("I"))
     act(R("rZT0", 512, 768), R("P2", 0, 256))
-    rot = [0]
 
     def spread(src, off, c):
-        bk = "P%d" % (rot[0] % 3)
-        rot[0] += 1
+        bk = ("P1", "P2", "P1", "P2", "P0", "P1", "P2", "P0")[c]
         b, q = divmod(c, 4)
         mm(R(bk), R(src, off + 128 * b, off + 128 * b + 128, 1, 32 * q, 32 * q + 32), R("EXP", 0, 512, 1, 32 * q, 32 * q + 32))
         return R(bk)
@@ -331,10 +338,9 @@ def plan(T, g, topo, core, rank):
         act(R("EV"), ind(EW, R(VL, 0, 16)))
         mm(R(D[1], 0, 256), R("DME"), R("EV"), True, False); mm(R(D[1], 0, 256), R("I3"), R(FV), False, True)
         act(R("PQ", 256, 512), R(D[1], 0, 256), bias=col(10 + t))
-        if last:
-            for c in range(4):
-                mm(R(K[c % 2]), R("WY"), bl("E", c, 0, 512))
-                act(bl("YT", c, 0, 512), R(K[c % 2]))
+        if t:
+            for b in range(2):
+                mm(bl("P0", b), bl(ZT, b), R("I"))
         for c in range(8):
             gather(bl("F", c, 0, 512), EW, bl("NL", c, 0, 32), c in FDVE)
         for b in range(2):
@@ -346,12 +352,15 @@ def plan(T, g, topo, core, rank):
             mm(R(D[b], 128, 256), bl("ETS", b), R("I3"), True, False)
             mm(R(D[b], 128, 256), bl("ST", b), R("N2I"), False, True)
             ts(bl("AL", b), R(D[b], 128, 256), 264192.0, A.add)
-            for c in range(4 * b, 4 * b + 4):
-                if t == 0:
+            mm(R(D[b], 384, 512), bl("ST", b), R("I"))
+            act(bl("SG", b), R(D[b], 384, 512), bias=-129.0)
+            if t == 0:
+                for c in range(4 * b, 4 * b + 4):
                     ts(bl("CM", c, 0, 512), bl("F", c, 0, 512), 2048.0, A.is_ge)
-                else:
-                    tt(bl("CM", c, 0, 512), bl("F", c, 0, 512), spread(ZT, 0, c), A.is_ge)
-                chain("c")
+            else:
+                for k in range(16):
+                    s = (2048 * b + k, 2048 * b + 2048, 16)
+                    tt(R("CM", *s), R("F", *s), bl("P0", b), A.is_ge)
         for c in range(8):
             gather(bl("RW", c, 0, 512), R("X"), bl("AL", c, 0, 32), c in RDVE)
             tt(bl("MX", c, 0, 512), bl("RW", c, 0, 512), spread(ZT, 512, c), A.max)
@@ -376,10 +385,8 @@ def plan(T, g, topo, core, rank):
             tt(bl("WT", b), kb, bl("MB", b), A.is_equal)
             mm(R(D[b], 256, 384), bl("WT", b), R("I"))
             tt(bl("HUB", b), R(D[b], 256, 384), bl("PAY", b), A.mult)
-            tb = table(sOM, b, True)
-            tt(bl("TT", b, 0, 256), tb, bl(OM, b, 256, 256), A.add)
-            if not last:
-                act(bl(sOM, b, 256, 256), tb)
+            tt(bl("HS", b), R(D[b], 256, 384), bl("SG", b), A.mult)
+            table(sOM, b, True, OM, not last)
         for src in ("FF16", "HUB"):
             for l in range(16):
                 mm(R("P0", 0, 16), R("L", 128 * l, 128 * l + 128), R(src, l, 256, 16), src == "FF16" and l == 0, src == "HUB" and l == 15)
@@ -404,14 +411,15 @@ def plan(T, g, topo, core, rank):
         mm(R("P2", 0, 256), R("DMO"), R("EV"), True, False); mm(R("P2", 0, 256), R("G15"), R("FF16"), False, False)
         mm(R("P2", 0, 256), R("G15"), R("HUB"), False, True)
         act(R("PQ", 0, 256), R("P2", 0, 256), bias=col(10 + t))
-        act(R("MI"), R("MB"), bias=col(28))
-        act(R("MJ"), R("MI"), bias=col(28), scale=-1.0)
-        mm(R(K[1], 256, 512), R("I3"), R("MB"), True, False); mm(R(K[1], 256, 512), R("I3"), R("MJ"), False, True)
-        act(R(sZT, 0, 256), R(K[1], 256, 512), bias=col(29), scale=2048.0)
         for b in range(2):
-            mm(bl("P1", b), bl("MB", b), R("I3"))
-        act(R("NFS"), R("P1", 0, 256), AF.Relu, bias=col(27), acc=None if last else R("NFC"))
-        tt(R("XN"), ind(R("X"), FL), R("NFS"), A.mult)
+            mm(bl(K[1], b, 256), bl("HS", b), R("GO"))
+        act(R(sZT, 0, 256), R(K[1], 256, 512), bias=2048.0, scale=2048.0)
+        act(R("XR"), ind(R("X"), FL))
+        mm(R("P1", 0, 256), R("I"), R("XR"), True, False)
+        mm(R("P1", 0, 256), R("NG"), R("HS"), False, True)
+        act(R("XN"), R("P1", 0, 256), AF.Relu)
+        if not last:
+            act(R("NFS"), R(sZT, 0, 256), AF.Relu, bias=2.0, scale=-1.0 / 2048, acc=R("NFC"))
         o1 = R("P1", 0, 256)
         mm(o1, R("G15"), R("FF16"), True, False); mm(o1, R("G15"), R("HUB"), False, not last)
         if last:
@@ -425,10 +433,13 @@ def plan(T, g, topo, core, rank):
         if last:
             act(R(sZT, 256, 512), o1, AF.Abs)
             dma(lambda s=sZT: T.yz[:], lambda s=sZT: T[s][:, 256:512], [], [R(sZT, 256, 512)], 2200)
-            mm(R("P2"), R("WY"), R("GF"), True, False); mm(R("P2"), R("WY"), R("PQ"), False, True)
-            act(R("YN"), R("P2"))
-            cp(ind(R("YT"), R("SL")), R("YN"))
-            dma(lambda: T.ys[:], lambda: T.YT[0:128:16, 0:2048], [], [R("YT")], 2200)
+            tt(ind(R("E"), R("SL")), R("GF"), R("PQ"), A.add)
+            for c in range(16):
+                mm(R("P2", c, 128, 16), bl("E", c), R("WY"))
+            cp(R("YN"), R("P2", 0, 128))
+            mm(R("P0", 0, 128), R("YN"), R("I3"))
+            cp(R("YT"), R("P0", 0, 128))
+            dma(lambda: T.ys[:], lambda: T.YT[:], [], [R("YT")], 2000)
         else:
             for b in range(2):
                 o = bl("P1", b, 256)
@@ -457,13 +468,13 @@ def schedule(ops):
             for r in rs:
                 ps = r[0] not in SB
                 a, b, st = (0, 512, 1) if ps else (r[1], r[2], r[3])
-                x = wr or ps
+                x = wr
                 h = hist.setdefault(r[0], [])
                 for (j, c, d, y, s2) in h:
-                    if j != i and c < b and a < d and (x or y) and not (st == s2 and (a - c) % st):
+                    if j != i and c < b and a < d and (x or y or (ps and ops[j]["q"] != o["q"])) and not (st == s2 and (a - c) % st):
                         dep.add(j)
-                if x and st == 1:
-                    h[:] = [e for e in h if not (a <= e[1] and e[2] <= b)]
+                if x:
+                    h[:] = [e for e in h if not (a <= e[1] and e[2] <= b and (st == 1 or (e[4] == st and a == e[1])))]
                 h.append((i, a, b, x, st))
         o["dep"] = dep
     n = len(ops)
@@ -545,6 +556,26 @@ def schedule(ops):
             cur = (end, st)
         if end < best[0]:
             best = (end, st)
+    names = {}
+    grp = []
+    for o in ops:
+        k = (o["q"], (o["w"] or o["r"])[0][0].rstrip("0123"), o["r"][0][0].rstrip("0123") if o["r"] else "", (o["w"] or o["r"])[0][1] >= 128)
+        grp.append(names.setdefault(k, len(names)))
+    off = [0.0] * len(names)
+    base = list(best[1])
+    for it in range(GROUPS):
+        new = list(off)
+        for m in range(1 + it % 2):
+            rs = (rs * 1103515245 + 12345) % 2147483648
+            k = (rs >> 8) % len(names)
+            rs = (rs * 1103515245 + 12345) % 2147483648
+            new[k] += (rs / 2147483648.0 - 0.5) * (8000.0 if it % 3 else 2000.0)
+        st = place([base[i] + new[grp[i]] for i in range(n)], pred, suc, False)
+        end = max(st[i] + ops[i]["c"] for i in range(n))
+        if end <= best[0] + 1:
+            best, off = (end, st), new
+        if it % 250 == 249:
+            base, off = list(best[1]), [0.0] * len(names)
     st = best[1]
     for i in range(n):
         ops[i]["t"] = (st[i], st[i] + ops[i]["c"])

@@ -3,48 +3,55 @@ from concourse.mybir import AluOpType as A, ActivationFunctionType as AF
 
 HOPS, STEP = 4, 3
 F32, BF, F16, I32, U16 = "float32", "bfloat16", "float16", "int32", "uint16"
+DIAG = ("I", "NI", "N2I", "BI", "I29", "I21", "N16", "I7", "N7", "N32")
 SB = {
     "ENI": (2048, I32), "E": (2560, F32), "X": (2048, BF), "YT": (128, F32), "V0": (16, I32), "WTI": (1, I32),
-    "F": (4096, F32), "CM": (4096, BF), "RW": (4096, BF), "MX": (4096, BF), "RH": (2048, BF),
-    "L": (2048, BF), "EXP": (512, BF), "Q0": (512, BF), "Q1": (128, F32), "Q2": (128, F32), "Q3": (128, F32),
-    "PI": (4, I32), "COL": (42, F32), "I": (128, BF), "NI": (128, BF), "N2I": (128, BF), "BI": (128, BF), "I3": (128, F32),
-    "GO": (128, BF), "WG": (128, BF), "WY": (8, F32), "G15": (128, BF), "DMO": (128, F32), "DME": (128, F32),
-    "C16": (128, F32), "DG": (128, F32), "CW": (128, BF), "G8": (24, BF), "KC": (128, BF), "TH": (128, F32),
-    "CR": (128, F32), "K16": (256, BF), "IOT": (128, BF), "THR": (16, F32), "DUM": (32, F32),
-    "ZER": (256, BF), "CX": (128, BF), "HY": (16, F32), "OT": (256, BF), "KI": (256, F32), "GI": (128, F32), "ONE": (128, BF),
-    "R32": (256, I32), "RN": (256, I32), "NL": (256, U16), "EV": (256, F32), "ETS": (256, F32), "ST": (256, BF),
-    "AL": (256, U16), "PAY": (256, F16), "VT": (256, BF), "SS": (320, F32), "MB": (256, F32), "WT": (256, BF),
-    "HUB": (256, F16), "SG": (256, BF), "HS": (256, BF), "NG": (128, BF), "NFS": (256, BF),
-    "AI": (2, I32), "UH": (256, BF), "SQ": (256, F32), "QI": (256, I32), "QJ": (256, I32),
-    "FFB": (256, F32), "FF16": (256, F16), "NF32": (32, F32), "DV": (32, F32), "HT": (16, F32), "LK": (32, I32),
-    "LW": (384, BF), "TT": (512, BF), "G": (512, BF), "NS": (16, F32), "TS": (32, F32), "OS": (32, F32), "SL": (32, U16),
+    "F": (4096, F32), "RW": (4096, BF), "MX": (4096, BF), "RH": (2048, BF),
+    "LT": (240, BF), "EXP": (512, BF), "NEX": (512, BF), "Q0": (512, BF), "Q1": (128, F32), "Q3": (128, F32),
+    "PI": (8, I32), "COL": (42, F32), "DG": (128 * len(DIAG), BF), "I3": (256, F32), "E0": (128, BF), "AH": (1, BF), "WB": (1, BF),
+    "CI0": (256, BF), "CM": (4096, BF), "CW": (384, BF), "W8": (8, BF), "WY": (8, F32), "DMO": (128, F32), "DME": (128, F32),
+    "C16": (128, F32), "G8": (64, BF), "KC": (768, BF), "KP": (384, BF), "RS": (384, F32), "DUM": (128, F32),
+    "K16": (256, BF), "I16": (128, BF), "IOT": (128, BF), "SPL": (8, U16), "SPH": (8, U16), "V0F": (32, F32),
+    "ZER": (256, BF), "M": (48, F32), "HY": (48, F32), "OT": (256, BF), "KI": (384, F32), "GI": (128, F32), "ONE": (128, BF),
+    "R32": (256, I32), "RN": (256, I32), "NL": (256, U16), "EV": (256, F32), "RND": (512, F32), "FR": (512, BF), "ST": (256, BF),
+    "ENT": (256, F32), "UP": (256, F16), "AL": (256, U16), "VT": (256, BF), "SS": (768, F32), "NFS": (16, BF),
+    "UH": (16, BF), "SQ": (16, F32), "QI": (16, I32), "QJ": (32, I32), "FK": (48, F32),
+    "RM": (256, F16), "SM": (256, F16), "CF": (32, F32), "XS": (32, F32),
+    "LW": (256, BF), "TT": (512, BF), "G": (512, BF), "SL": (32, U16),
     "GF": (512, F32), "PQ": (512, F32), "XN": (256, BF), "XR": (256, BF), "YN": (128, F32), "YP": (256, F32),
 }
 for _t in range(HOPS):
+    SB["PL%d" % _t] = (48, F32)
     for _s in ("r", "s"):
         SB["%sVL%d" % (_s, _t)] = (32, U16)
         SB["%sZT%d" % (_s, _t)] = (768, BF)
         SB["%sOM%d" % (_s, _t)] = (768, BF)
-        SB["%sF%d" % (_s, _t)] = (256, F32)
-del SB["sF3"]
+        SB["%sW%d" % (_s, _t)] = (768, BF)
 SCRATCH = {k: ("sbuf", [128, v[0]], v[1]) for k, v in SB.items()}
 for _b in range(8):
     SCRATCH["P%d" % _b] = ("psum", [128, 512], F32)
-SEMAPHORES = ["v", "s", "p", "gq", "sent"] + ["d%d" % i for i in range(11)] + ["a%d" % i for i in range(15)]
+SEMAPHORES = ["v", "s", "p", "gq", "sent"] + ["d%d" % i for i in range(11)] + ["a%d" % i for i in range(21)]
 
 CY, PE, LAT, GA, SC = 1.0, 0.5, 140.0, 1.56, 3.5
-COM, GROUPS = 2000, 500
-SEARCH, ROUNDS = 300, 4
-FDVE, RDVE = (2, 3), ()
-TH0 = 655360.0 - 6
+COM, GROUPS = 800, 200
+SEARCH, ROUNDS, LOCAL = 50, 4, 8000
+FDVE = ((0, 1, 4, 5), (2, 3, 5), (2, 3, 5), (2, 3, 5))
+RDVE = ((0, 5), (), (), ())
+MSC = ((), (), (), ())
+TTV, STV = False, False
+FAIL = 9 * 2 ** 20
+MARK = 2048 - 31.0 / 32
 NUM = {30: 1.0, 20: 100 * math.log(2.0), 21: 100 * math.log(2.0) + math.log(3.5), 22: 129 - 1023.5 / 2048, 23: 592.0 + 264192,
-       24: -2048.0, 31: -63.5, 32: 8 * 2.0 ** 20 + TH0, 33: 32768.0}
+       24: -2048.0, 33: 32768.0}
 
 
 def R(n, a=0, b=None, st=1, p0=0, p1=128):
     if n in ("NFC", "ACOL"):
         a = 36 if n == "NFC" else 37
         return ("COL", a, a + 1, 1, 0, 128)
+    if n in DIAG:
+        o = 128 * DIAG.index(n)
+        return ("DG", o + a, o + (128 if b is None else b), st, p0, p1)
     if b is None:
         b = SB[n][0] if n in SB else 512
     return (n, a, b, st, p0, p1)
@@ -137,6 +144,12 @@ def plan(T, g, topo, core, rank):
         else:
             f = lambda: g.iota(ap(o), pat, base, cm, allow_small_or_imprecise_dtypes=True)
         add("gq", f, [o], [], 130 + 2 * ne(o) * CY)
+
+    def fill(o, c):
+        iota(o, [[0, ne(o)]], c, 0)
+
+    def sel(o, pat, op, c, base, cm):
+        add("gq", lambda: g.affine_select(ap(o), ap(o), pat, op, c, base, cm), [o], [o], 170 + 2 * ne(o) * CY)
     nd = [0]
 
     def dma(o, a, out, ins, cost):
@@ -172,132 +185,155 @@ def plan(T, g, topo, core, rank):
     dma(lambda: T.rZT0[:, 256:512], lambda: T.z0[:], [R("rZT0", 256, 512)], [], 5800)
     dma(lambda: T.WTI[:], lambda: T.wt[:], [R("WTI")], [], 5900)
     dma(lambda: T.X[:], lambda: T.xs[:], [R("X")], [], 7500)
+    I3 = R("I3", 0, 128)
     iota(R("PI", 0, 1), [[1, 1]], 0, 1)
-    iota(R("KI"), [[0, 16], [1, 16]], 0, 0)
-    iota(R("GI"), [[1, 8], [0, 16]], 0, 0)
-    iota(R("Q1"), [[1, 128]], 0, -1)
+    iota(R("KI", 0, 128), [[0, 8], [1, 16]], 0, 0)
     iota(R("Q3"), [[0, 16], [1, 8]], 0, 0)
+    iota(R("Q1"), [[1, 128]], 0, -1)
     iota(R("IOT"), [[1, 128]], 0, 0)
+    fill(R("rW0", 0, 640), 0)
+    iota(R("GI"), [[1, 8], [0, 16]], 0, 0)
+    fill(R("ZER"), 0); fill(R("ONE"), 1); fill(R("C16"), 1)
+    iota(R("KI", 128, 384), [[0, 16], [1, 16]], 0, 0)
     iota(R("Q0"), [[1, 32], [0, 16]], 0, 0)
-    iota(R("Q2"), [[1, 16], [16, 8]], 0, -1)
-    iota(R("DUM"), [[1, 32]], 2048, 0)
-    iota(R("THR"), [[0, 2], [16, 8]], 0, 0)
-    iota(R("L"), [[0, 2048]], 0, 0)
-    cp(col(0), R("PI", 0, 1))
-    ts(R("PI", 1, 2), R("PI", 0, 1), 15, A.bitwise_and); cp(col(1), R("PI", 1, 2))
-    ts(R("PI", 2, 3), R("PI", 0, 1), 4, A.arith_shift_right); cp(col(2), R("PI", 2, 3))
-    ts(R("PI", 3, 4), R("PI", 0, 1), 1, A.bitwise_and); cp(col(14), R("PI", 3, 4))
-    ts(col(6), col(1), 15.0, A.is_equal)
-    tt(col(4), col(14), col(6), A.subtract)
-    ts(R("PI", 3, 4), R("PI", 0, 1), 31, A.bitwise_and); cp(col(15), R("PI", 3, 4))
-    ts(col(16), col(15), 16.0, A.is_ge, 128.0, A.mult)
-    ms(col(19), 1e29)
-    act(col(5), col(14), bias=col(30), scale=-1.0)
+    fill(R("RS"), 0); fill(R("RS", 0, 384, 16), 2 ** 24 - 1); fill(R("FK", 32, 48), FAIL)
+    for j, c in enumerate((131072, 1040, -129)):
+        fill(bl("KP", j), c)
+    iota(R("DUM"), [[0, 8], [256, 2], [0, 8]], 2048, 2)
+    sel(R("DUM"), [[0, 16], [-16, 8]], A.is_ge, 0.0, 0, 1); sel(R("DUM"), [[0, 16], [16, 8]], A.is_ge, 0.0, 15, -1)
+    fill(R("CW"), 65536)
+    sel(R("CW"), [[0, 3], [-16, 8], [0, 16]], A.is_ge, 0.0, 0, 1); sel(R("CW"), [[0, 3], [16, 8], [0, 16]], A.is_ge, 0.0, 15, -1)
+    sel(R("CW"), [[0, 3], [-1, 128]], A.not_equal, 2.0 ** 24, 0, 1)
     for t in range(HOPS):
-        act(col(10 + t), col(6), scale=2048.0 * (9 + t))
-    act(col(17), col(1), bias=col(30))
-    act(col(18), col(1), scale=32.0)
-    act(col(8), col(19), scale=1e4)
-    ts(R("WT"), R("KI"), col(1), A.is_equal); cp(R("SL", 0, 16), R("KI", 0, 16))
-    ts(R("I3"), R("Q1"), 0.0, A.is_equal)
-    for n, c in (("I", 1.0), ("NI", -1.0), ("N2I", -2048.0), ("BI", 512.0), ("DMO", col(4)), ("DME", col(5))):
-        act(R(n), R("I3"), scale=c)
-    ts(R("EXP"), R("Q0"), col(15), A.is_equal)
-    ts(R("GO"), R("GI"), col(2), A.is_equal)
-    act(R("NG"), R("GO"), scale=-64.0)
-    cp(col(3), R("WTI"))
-    act(R("WG"), R("GO"), scale=col(3))
+        fill(R("sW%d" % t), 0)
+    p = R("PI", 0, 1)
+    for j, (sh, m) in enumerate(((0, 15), (4, 7), (0, 1), (0, 31), (4, 1), (0, 8))):
+        ts(R("PI", j + 1, j + 2), p, sh, A.arith_shift_right, m, A.bitwise_and)
+    cp(R("COL", 0, 7), R("PI", 0, 7))
+    act(col(18), col(1), AF.Relu, bias=-14.0)
+    act(col(14), col(18), bias=col(3), scale=-1.0)
+    act(col(15), col(3), bias=col(30), scale=-1.0)
+    act(col(16), col(5), scale=128.0)
+    ms(col(8), 1e29)
+    for t in range(HOPS):
+        act(col(10 + t), col(18), scale=2048.0 * (9 + t))
+    ts(R("SPL"), R("KI", 0, 8), col(6), A.add)
+    ts(R("SPH"), R("KI", 0, 8), 16.0, A.mult, 15.0, A.add)
+    ts(I3, R("Q1"), 0.0, A.is_equal)
+    for n, c in (("I", 1.0), ("NI", -1.0), ("N2I", -2048.0), ("BI", 8192.0), ("DMO", col(14)), ("DME", col(15)), ("I29", 2.0 ** 29),
+                 ("I21", 2.0 ** 21), ("N16", -16.0), ("I7", 128.0), ("N7", -128.0), ("N32", -1.0 / 32)):
+        act(R(n), I3, scale=c)
+    act(R("E0"), R("ONE"), scale=R("I3", 0, 1))
+    ts(R("EXP"), R("Q0"), col(4), A.is_equal)
+    if any(MSC):
+        act(R("NEX"), R("EXP"), scale=-1.0)
+    ts(R("I3", 128, 256), R("GI"), col(2), A.is_equal)
+    cp(col(25), R("WTI"))
     ts(R("Q3"), R("Q3"), col(2), A.is_equal)
+    act(R("W8"), R("Q3", 0, 8), scale=col(25))
+    act(col(17), col(1), bias=col(30))
     act(R("WY"), R("Q3", 0, 8), scale=col(17))
-    for j, c in enumerate((512.0, -256.0)):
-        act(R("G8", 8 * j + 8, 8 * j + 16), R("Q3", 0, 8), scale=c)
-    act(R("G15"), R("GO"), scale=0.0); act(R("G15", 15, 128, 16), R("Q3", 0, 8))
-    ms(R("ONE"), 1.0); ms(R("ZER"), 0.0); ms(R("SS", 128, 160), 0.0); ms(R("SS", 288, 320), 0.0)
-    act(R("C16"), R("ONE"), scale=1.0 / 16)
-    for j in range(8):
-        act(R("L", 16 * j, 16 * j + 129 * 15 + 1, 129), R("ONE", 0, 16), scale=R("Q3", j, j + 1))
-    ts(R("DG"), R("Q2"), 0.0, A.is_equal)
-    act(R("Q2"), R("DG"), scale=4096.0 - 2.0 ** 20)
-    act(R("Q1"), R("Q3"), scale=-4096.0)
-    tt(R("CW"), R("Q2"), R("Q1"), A.add)
-    act(R("TH"), R("GI"), bias=col(32), scale=-2.0 ** 20)
-    for j, p, c in ((38, 0, -2.0 ** 20), (39, 1, 16.0), (40, 2, -4096.0), (41, 3, -135.0)):
-        ts(col(j), col(0), float(p), A.is_equal, c, A.mult)
-    act(col(34), col(38), bias=col(40), scale=-9.0); act(col(34), col(34), bias=col(41))
-    act(R("MB", 0, 128), R("KI", 0, 128), bias=col(34), scale=col(39))
-    act(R("GI"), R("GI"), scale=col(38))
-    tt(R("KC"), R("MB", 0, 128), R("GI"), A.add)
-    ts(R("CR"), R("KI", 0, 128), 1.0, A.min, 2e9, A.mult)
-    act(R("K16"), R("KI"), bias=col(33), scale=-2048.0)
-    act(R("DUM"), R("DUM"), bias=col(18))
-    act(R("THR"), R("THR"), bias=col(1))
+    act(R("G8", 0, 16), R("Q3", 0, 16))
+    act(R("G8", 16, 40), R("Q3", 0, 24), scale=8192.0)
+    act(R("G8", 40, 64), R("Q3", 0, 24), scale=-4096.0)
+    ms(R("CI0"), 2.0 ** -9)
+    ms(R("LT"), 0.0); ts(R("LT", 112, 128), R("KI", 0, 16), col(1), A.is_equal)
+    act(col(39), R("I3", 1, 2), scale=256.0); act(col(34), R("I3", 0, 1), scale=-7 * 2.0 ** 24)
+    act(bl("KC", 0, 0, 384), R("KI"), bias=col(34), scale=col(39))
+    act(bl("KC", 1, 0, 384), R("KI"), scale=col(39))
+    act(R("K16"), R("KI", 0, 256), bias=col(33), scale=-2048.0)
+    act(R("I16"), R("KI", 0, 128))
     act(col(7), col(0), AF.Exp, bias=col(20), scale=-math.log(3.0))
-    act(R("THR"), R("THR"), AF.Exp, bias=col(21), scale=-math.log(3.0))
+    act(col(9), col(0), AF.Exp, bias=col(21), scale=-math.log(3.0))
     ops[-1]["c"] = ops[-1]["busy"] = 100
-    ts(col(25), col(0), 0.0, A.is_equal, -128.0, A.mult); ts(col(26), col(0), 1.0, A.is_equal, -63.5, A.mult)
-    ts(R("CX"), R("KI", 0, 128), col(25), A.mult, col(26), A.add)
-    act(R("IOT"), R("IOT"), bias=col(31))
-    ms(R("ACOL"), -350464.0)
+    act(col(19), col(8), scale=1e4); act(R("WB"), col(7))
+    act(R("ACOL"), col(0), bias=-350464.0, scale=0.0)
     for c in range(4):
         cp(bl("E", c, 0, 512), bl("ENI", c, 0, 512))
     D, K, FM = ("P3", "P4"), ("P5", "P6"), "P7"
-    MAG = 1.5 * 2.0 ** 30
+    MAG1, MAG2 = 1.5 * 2.0 ** 23, 1.5 * 2.0 ** 31
 
-    def table(OM, b, ff, base=None, pure=True):
-        x = R(K[b], 128, 256)
-        mm(x, R("ONE"), R("CX"), True, False)
-        if ff:
-            mm(x, bl("FF16", b), R("GO"), False, False)
-        mm(x, bl("HUB", b), R("GO"), False, True)
-        x0 = R(K[b], 128, 256, 16)
-        ts(bl("HY", b, 0, 8), x0, MAG, A.add, -MAG, A.add)
-        ts(bl("OT", b), x, MAG, A.add, MAG, A.is_equal)
-        tt(bl("HT", b, 0, 8), x0, bl("HY", b, 0, 8), A.subtract)
-        act(bl("LW", b), bl("OT", b), scale=col(7))
+    def wp(W, b, j, n=1):
+        return R(W, 384 * b + 128 * j + 15, 384 * b + 128 * (j + n), 16)
+
+    def wt(W, b, j):
+        return R(W, 384 * b + 128 * j, 384 * b + 128 * j + 128)
+
+    def tolist(buf, b, win, mask, op, o):
+        tt(bl(buf, b), ind(win, R("SPL")), mask, op)
+        for a in range(8):
+            mm(o, R("LT", 112 - 16 * a, 240 - 16 * a), R(buf, 128 * b + 16 * a, 128 * b + 16 * a + 16), a == 0, a == 7)
+
+    def table(OM, VL, W, PL, b, base=None, pure=True):
+        mm(R(D[b], 136, 144), R("I"), wp(W, b, 0))
+        mm(R(D[b], 128, 136), R("I"), wp(W, b, 0), True, False); mm(R(D[b], 128, 136), R("I7"), wp(W, b, 1), False, True)
+        if base:
+            act(R(PL, 24 * b + 8, 24 * b + 24), R(D[b], 128, 144))
+        else:
+            act(R(PL, 24 * b, 24 * b + 8), R(D[b], 128, 136))
+        tt(bl("OT", b), ind(wt(W, b, 1), R("SPH")), R("I16"), A.is_equal)
         if b == 0:
-            act(R("LW", 256, 384), bl("OT", 0), scale=col(8))
-        for c in range(8 * b, 8 * b + 8):
-            ts(bl("RH", c), R("IOT"), R("HT", c, c + 1), A.is_equal)
+            act(bl("LW", 0), bl("OT", 0), scale=col(7))
+            act(bl("LW", 1), bl("OT", 0), scale=col(19))
+        if base:
+            tolist("RM", b, R(PL, 24 * b + 8, 24 * b + 24), R("Q3"), A.mult, R(D[b], 144, 160))
+            ts(bl(VL, b, 16, 8), R(D[b], 152, 160), col(16), A.add, 256.0 * b, A.add)
+            cp(bl(VL, b, 0, 8), R(D[b], 144, 152))
+        for c in range(8):
+            lo = R(W, 384 * b + 16 * c + 15, 384 * b + 16 * c + 16)
+            if b:
+                ts(bl("RH", 8 + c), R("IOT"), lo, A.is_equal, R("WB"), A.mult)
+            else:
+                ts(bl("RH", c), R("IOT"), lo, A.is_equal)
         mm(R(D[b], 384, 512), bl("OT", b), R("I"))
         act(bl(OM, b), R(D[b], 384, 512))
+        both = base and pure and not TTV
+        bk = FM if b else K[0]
 
-        def sums(k0, k1, s0, s1, d0, d1):
-            if b == 0:
-                mm(R(k1, 0, 256), R("I"), s1, True, False)
-                mm(R(k0, 256, 512), R("I"), s0, True, False)
+        def sums(bank, c0, l, l0, stop):
             for a in range(4):
-                r = R("RH", 1024 * b + 256 * a, 1024 * b + 256 * a + 256)
-                o1 = R(k1, 0, 256, 1, 32 * a, 32 * a + 32)
-                if b == 0:
-                    mm(R(k0, 256, 512, 1, 32 * a, 32 * a + 32), R("LW", 32 * a, 32 * a + 32), r, False, True)
-                    mm(o1, R("LW", 256 + 32 * a, 288 + 32 * a), r, False, False)
-                else:
-                    mm(o1, R("LW", 128 + 32 * a, 160 + 32 * a), r, False, True)
-            act(d1 if b else d0, R(k1, 0, 256) if b else R(k0, 256, 512))
-        if base:
-            sums(K[0], FM, R(base, 256, 512), R(base, 512, 768), R("TT", 0, 256), R("TT", 256, 512))
-        if pure:
-            sums(K[0], D[0], R("ZER"), R("ZER"), R(OM, 256, 512), R(OM, 512, 768))
-
-    def look(VL, src):
-        cp(R("LK", 0, 16), src)
-        ts(R("LK", 16, 32), R("LK", 0, 16), 127, A.bitwise_and)
+                mm(R(bank, c0, c0 + 256, 1, 32 * a, 32 * a + 32), R(l, l0 + 32 * a, l0 + 32 * a + 32),
+                   R("RH", 1024 * b + 256 * a, 1024 * b + 256 * a + 256), False, stop)
+        first = [bl(base, x, 256, 256) if both or not pure else R("ZER", 0, 256) for x in range(2)]
+        if b == 0:
+            mm(R(K[0], 0, 256), R("I"), first[0], True, False)
+            mm(R(FM, 0, 256), R("I"), first[1], True, False)
+        sums(bk, 0, "OT" if b else "LW", 128 * b, True)
+        if both or not pure:
+            act(bl("TT", b, 0, 256), R(bk, 0, 256))
+        if b == 0:
+            sums(FM, 0, "LW", 128, False)
+        if both:
+            if b == 0:
+                mm(R(K[0], 256, 512), R("I"), R("ZER", 0, 256), True, False)
+            sums(K[0], 256 - 256 * b, "OT" if b else "LW", 128 * b, True)
+            act(bl(OM, b, 256, 256), R(K[0], 256 - 256 * b, 512 - 256 * b))
+            if b == 0:
+                mm(R(K[0], 0, 256), R("I"), R("ZER", 0, 256), True, False)
+                sums(K[0], 0, "LW", 128, False)
+        elif pure:
+            if base:
+                tt(bl("TT", b, 0, 256), R(bk, 0, 256), bl(base, b, 256, 256), A.add)
+            act(bl(OM, b, 256, 256), R(bk, 0, 256))
+    cp(R("rVL0", 0, 16), R("V0"))
+    ts(R("QJ", 0, 16), R("V0"), 127, A.bitwise_and); ts(R("QJ", 16, 32), R("V0"), 7, A.arith_shift_right)
+    cp(R("V0F"), R("QJ"))
+    for j in range(2):
+        tolist("RM", j, bl("V0F", j, 0, 16), R("Q3"), A.mult, R(K[j], 0, 16))
         for b in range(2):
-            ts(bl(VL, b, 16, 8), bl("LK", b, 16, 8), col(16), A.add, 256.0 * b, A.add)
-    cp(R("rVL0", 0, 16), R("V0")); cp(R("NF32", 16, 32), R("V0"))
-    tt(R("HUB"), ind(R("NF32", 16, 32), R("SL", 0, 16)), R("WT"), A.mult)
-    look("rVL0", R("V0"))
+            act(wp("rW0", b, j), bl(K[j], b, 0, 8))
     for b in range(2):
-        table("rOM0", b, False)
-    mm(R("P1", 0, 256), R("G15"), R("HUB")); act(R("rF0"), R("P1", 0, 256))
+        ts(bl("rVL0", b, 16, 8), bl("V0F", b, 0, 8), col(16), A.add, 256.0 * b, A.add)
+        table("rOM0", "rVL0", "rW0", "PL0", b)
     for b in range(2):
         mm(bl("P2", b), bl("rZT0", b, 256), R("I"))
     act(R("rZT0", 512, 768), R("P2", 0, 256))
 
-    def spread(src, off, c):
-        bk = ("P1", "P2", "P1", "P2", "P0", "P1", "P2", "P0")[c]
+    def spread(src, off, c, neg):
+        bk = ("P1", "P2", "P1", "P2", "P0", "P1", "P0", "P1")[c]
         b, q = divmod(c, 4)
-        mm(R(bk), R(src, off + 128 * b, off + 128 * b + 128, 1, 32 * q, 32 * q + 32), R("EXP", 0, 512, 1, 32 * q, 32 * q + 32))
+        mm(R(bk), R(src, off + 128 * b, off + 128 * b + 128, 1, 32 * q, 32 * q + 32),
+           R("NEX" if neg else "EXP", 0, 512, 1, 32 * q, 32 * q + 32), True, not neg)
         return R(bk)
     prev = {}
 
@@ -306,138 +342,156 @@ def plan(T, g, topo, core, rank):
         if key in prev:
             ops[-1]["seq"] = prev[key]
         prev[key] = len(ops) - 1
-
-    def gather(o, w, l, dve):
-        if dve:
-            cp(o, ind(w, l))
-        else:
-            act(o, ind(w, l))
-        chain("g")
     EW = R("E", 0, 2048)
     for t in range(HOPS):
         last = t == HOPS - 1
-        VL, ZT, OM, FV = "rVL%d" % t, "rZT%d" % t, "rOM%d" % t, "rF%d" % t
-        sVL, sZT, sOM, sF = "sVL%d" % t, "sZT%d" % t, "sOM%d" % t, "sF%d" % t
+        VL, ZT, OM, W, PL = "rVL%d" % t, "rZT%d" % t, "rOM%d" % t, "rW%d" % t, "PL%d" % t
+        sVL, sZT, sOM, sW = "sVL%d" % t, "sZT%d" % t, "sOM%d" % t, "sW%d" % t
         n = t + 1
         Z = R(ZT, 256, 512)
-        mm(R(FM, 0, 256), R("WG"), Z)
-        act(R("UH"), R(FM, 0, 256), bias=col(22), scale=1.0 / 2048)
-        mm(R(FM, 256, 512), R("WG"), Z, True, False); mm(R(FM, 256, 512), R("N2I"), R("UH"), False, True)
-        act(R("SQ"), R(FM, 256, 512), AF.Square, bias=col(23))
+        for b in range(2):
+            mm(R(FM, b, 16, 2), bl(ZT, b, 256), R("W8"))
+        act(R("UH"), R(FM, 0, 16), bias=col(22), scale=1.0 / 2048)
+        o = R(FM, 16, 32)
+        mm(o, R("N2I"), R("UH"), True, False)
+        for b in range(2):
+            mm(R(FM, 16 + b, 32, 2), bl(ZT, b, 256), R("W8"), False, b == 1)
+        act(R("SQ"), o, AF.Square, bias=col(23))
         ts(R("QI"), R("SQ"), R("ACOL"), A.add)
-        ts(R("QJ"), R("QI"), 5, A.arith_shift_right, 2047, A.bitwise_and)
-        ts(R("FFB"), R("QJ"), -264192.0, A.add); ts(R("FF16"), R("QJ"), 1.0 / 16, A.mult)
+        ts(R("QJ", 0, 16), R("QI"), 5, A.arith_shift_right, 127, A.bitwise_and)
+        ts(R("QJ", 16, 32), R("QI"), 12, A.arith_shift_right, 15, A.bitwise_and)
+        ts(R("FK", 0, 32), R("QJ"), float(FAIL), A.add)
         if t:
             mm(R(FM, 0, 256), R("I"), R(ZT, 0, 256), True, False); mm(R(FM, 0, 256), R("NI"), R("K16"), False, True)
             act(R("VT"), R(FM, 0, 256), AF.Relu)
-        cp(R("NF32", 0, 16), R(VL, 0, 16))
         for b in range(2):
             cp(bl("R32", b), ind(EW if t else R("ENI"), bl(VL, b, 0, 8)))
             ts(bl("RN", b), bl("R32", b), 2047, A.bitwise_and)
             cp(bl("NL", b), bl("RN", b))
         act(R("EV"), ind(EW, R(VL, 0, 16)))
-        mm(R(D[1], 0, 256), R("DME"), R("EV"), True, False); mm(R(D[1], 0, 256), R("I3"), R(FV), False, True)
-        act(R("PQ", 256, 512), R(D[1], 0, 256), bias=col(10 + t))
         if t:
             for b in range(2):
                 mm(bl("P0", b), bl(ZT, b), R("I"))
         for c in range(8):
-            gather(bl("F", c, 0, 512), EW, bl("NL", c, 0, 32), c in FDVE)
-        for b in range(2):
-            for k in range(16):
-                j = (k + t) % 16
-                mm(R(D[b], k, 128, 16), R("F", 2048 * b + k, 2048 * b + 2048, 16), R("DG", 8 * j, 8 * j + 8))
-            cp(bl("ETS", b), R(D[b], 0, 128))
-            ts(bl("ST", b), R(D[b], 0, 128), 1.0 / 2048, A.mult, 129 - 1023.5 / 2048, A.add)
-            mm(R(D[b], 128, 256), bl("ETS", b), R("I3"), True, False)
-            mm(R(D[b], 128, 256), bl("ST", b), R("N2I"), False, True)
-            ts(bl("AL", b), R(D[b], 128, 256), 264192.0, A.add)
-            mm(R(D[b], 384, 512), bl("ST", b), R("I"))
-            act(bl("SG", b), R(D[b], 384, 512), bias=-129.0)
-            if t == 0:
-                for c in range(4 * b, 4 * b + 4):
-                    ts(bl("CM", c, 0, 512), bl("F", c, 0, 512), 2048.0, A.is_ge)
+            o, a = bl("F", c, 0, 512), ind(EW, bl("NL", c, 0, 32))
+            if c in FDVE[t]:
+                if t:
+                    cp(o, a)
+                else:
+                    ts(o, a, MARK, A.max, -MARK, A.add)
+            elif t:
+                act(o, a)
             else:
+                act(o, a, AF.Relu, bias=-MARK)
+            chain("g")
+        for b in range(2):
+            o, cc, ent = R(D[b], 0, 256), R(D[b], 0, 128), bl("ENT", b)
+            if t:
+                for k in range(16):
+                    mm(R(D[b], k, 128, 16), R("F", 2048 * b + k, 2048 * b + 2048, 16), R("I3", (k + t) % 16, 128, 16))
+                act(ent, cc)
+                if STV:
+                    ts(bl("ST", b), cc, 1.0 / 2048, A.mult, 129 - 1023.5 / 2048, A.add)
+                else:
+                    act(bl("ST", b), cc, bias=col(22), scale=1.0 / 2048)
                 for k in range(16):
                     s = (2048 * b + k, 2048 * b + 2048, 16)
-                    tt(R("CM", *s), R("F", *s), bl("P0", b), A.is_ge)
-        for c in range(8):
-            gather(bl("RW", c, 0, 512), R("X"), bl("AL", c, 0, 32), c in RDVE)
-            tt(bl("MX", c, 0, 512), bl("RW", c, 0, 512), spread(ZT, 512, c), A.max)
-            chain("c")
-        for b in range(2):
-            tt(bl("PAY", b), R(D[b], 128, 256), bl("FFB", b), A.subtract)
-            kb = R(K[b], 0, 128)
-            mm(kb, R("ONE"), R("KC"), True, False)
-            if t:
-                mm(kb, R("BI"), bl("VT", b), False, False)
-            for src in ("CM", "ST", "RW", "MX"):
-                if src == "ST":
-                    mm(kb, R("I"), bl("ST", b), False, False)
-                    continue
+                    tt(R("CM", *s), R("F", *s), bl("P0", b), A.is_lt)
+            else:
+                mm(o, R("ONE"), R("CI0"), True, False)
                 for k in range(16):
-                    j = (k + t) % 16
-                    w = R("CW", 8 * j, 8 * j + 8) if src == "CM" else R("G8", 16, 24) if src == "RW" else R("G8", 8, 16)
-                    mm(R(K[b], k, 128, 16), R(src, 2048 * b + k, 2048 * b + 2048, 16), w, False, src == "MX" and k == 15)
-            s0 = 160 * b
-            scan(R("SS", s0, s0 + 128), R("TH"), kb, 1e9, A.min, A.min)
-            scan(bl("MB", b), R("CR"), R("SS", s0 + 15, s0 + 143), 0.0, A.min, A.max)
-            tt(bl("WT", b), kb, bl("MB", b), A.is_equal)
-            mm(R(D[b], 256, 384), bl("WT", b), R("I"))
-            tt(bl("HUB", b), R(D[b], 256, 384), bl("PAY", b), A.mult)
-            tt(bl("HS", b), R(D[b], 256, 384), bl("SG", b), A.mult)
-            table(sOM, b, True, OM, not last)
-        for src in ("FF16", "HUB"):
-            for l in range(16):
-                mm(R("P0", 0, 16), R("L", 128 * l, 128 * l + 128), R(src, l, 256, 16), src == "FF16" and l == 0, src == "HUB" and l == 15)
-        FL = R(sVL, 0, 16)
-        cp(FL, R("P0", 0, 16))
-        look(sVL, R("P0", 0, 16))
-        cp(R("NF32", 16, 32), FL)
-        tt(R("G", 0, 256), ind(R("TT"), R(VL, 16, 32)), R(OM, 0, 256), A.mult)
-        tt(R("G", 256, 512), ind(R("TT"), R(sVL, 16, 32)), R(sOM, 0, 256), A.mult)
-        for h in range(2):
-            for l in range(16):
-                mm(R(D[1], 0, 16), R("L", 128 * l, 128 * l + 128), R("G", 256 * h + l, 256 * h + 256, 16),
-                   h == 0 and l == 0, h == 1 and l == 15)
-        tt(R("DV"), R("DUM"), R("NF32"), A.subtract)
-        tt(R("NS"), R(D[1], 0, 16), R("THR"), A.is_ge)
-        for h in range(2):
-            tt(bl("TS", h, 0, 16), R("NS"), bl("DV", h, 0, 16), A.mult)
-        tt(R("OS"), R("TS"), R("NF32"), A.add)
-        cp(R("SL"), R("OS"))
-        act(R("GF", 0, 256), ind(EW, FL), scale=col(5))
-        act(R("GF", 256, 512), ind(EW, FL), scale=col(4))
-        mm(R("P2", 0, 256), R("DMO"), R("EV"), True, False); mm(R("P2", 0, 256), R("G15"), R("FF16"), False, False)
-        mm(R("P2", 0, 256), R("G15"), R("HUB"), False, True)
-        act(R("PQ", 0, 256), R("P2", 0, 256), bias=col(10 + t))
+                    mm(R(D[b], k, 256, 16), R("F", 2048 * b + k, 2048 * b + 2048, 16), R("I3", k, 256, 16), False, k == 15)
+                ts(bl("RND", b, 0, 256), o, MAG1, A.add, -MAG1, A.add)
+                act(bl("ST", b), bl("RND", 2 * b), bias=129 + 1023.5 / 2048, scale=1.0 / 2048)
+                act(ent, bl("RND", 2 * b), bias=2047.0)
+                tt(bl("FR", b, 0, 256), o, bl("RND", b, 0, 256), A.subtract)
+            o = R(D[b], 256, 384)
+            mm(o, ent, I3, True, False)
+            mm(o, bl("ST", b), R("N2I"), False, True)
+            ts(bl("AL", b), o, 264192.0, A.add)
+            ts(bl("UP", b), ent, 1.0 / 128, A.mult, 1024 - 63.5 / 128, A.add)
         for b in range(2):
-            mm(bl(K[1], b, 256), bl("HS", b), R("GO"))
-        act(R(sZT, 0, 256), R(K[1], 256, 512), bias=2048.0, scale=2048.0)
-        act(R("XR"), ind(R("X"), FL))
-        mm(R("P1", 0, 256), R("I"), R("XR"), True, False)
-        mm(R("P1", 0, 256), R("NG"), R("HS"), False, True)
-        act(R("XN"), R("P1", 0, 256), AF.Relu)
-        if not last:
-            act(R("NFS"), R(sZT, 0, 256), AF.Relu, bias=2.0, scale=-1.0 / 2048, acc=R("NFC"))
+            kb = R(K[b], 0, 384)
+            mm(kb, R("ONE"), bl("KC", min(t, 1), 0, 384), True, False)
+            if t:
+                for k in range(16):
+                    mm(R(K[b], k, 384, 16), R("CM", 2048 * b + k, 2048 * b + 2048, 16), R("CW", (k + t) % 16, 384, 16), False, False)
+            for j in range(3):
+                if t:
+                    mm(bl(K[b], j), R("BI"), bl("VT", b), False, False)
+                else:
+                    mm(bl(K[b], j), R("I29"), bl("FR", 2 * b), False, False)
+                    mm(bl(K[b], j), R("I21"), bl("FR", 2 * b + 1), False, False)
+            mm(kb, R("E0"), R("KP"), False, False)
+            for j, l, r in ((0, I3, "ENT"), (0, R("N7"), "UP"), (1, R("I"), "UP"), (1, R("N16"), "ST"), (2, R("I"), "ST")):
+                mm(bl(K[b], j), l, bl(r, b), False, False)
+            for c in range(4 * b, 4 * b + 4):
+                o, a, x = bl("RW", c, 0, 512), ind(R("X"), bl("AL", c, 0, 32)), bl("MX", c, 0, 512)
+                if c in RDVE[t]:
+                    cp(o, a)
+                else:
+                    act(o, a)
+                chain("g")
+                z = spread(ZT, 512, c, c in MSC[t])
+                if c in MSC[t]:
+                    mm(z, R("I"), o, False, True)
+                    act(x, z, AF.Relu)
+                else:
+                    tt(x, o, z, A.max)
+                chain("c")
+            for src in ("RW", "MX"):
+                for k in range(16):
+                    mm(R(K[b], k, 384, 16), R(src, 2048 * b + k, 2048 * b + 2048, 16),
+                       R("G8", 40, 64) if src == "RW" else R("G8", 16, 40), False, src == "MX" and k == 15)
+            scan(bl("SS", b, 0, 384), R("RS"), kb, 0.0, A.add, A.min)
+            m, hy = bl("M", b, 0, 24), bl("HY", b, 0, 24)
+            tt(m, R("SS", 384 * b + 15, 384 * b + 384, 16), R("FK", b, 48, 2), A.min)
+            ts(hy, m, MAG2, A.add, -MAG2, A.add)
+            tt(wp(sW, b, 0, 3), m, hy, A.subtract)
+            table(sOM, sVL, sW, PL, b, OM, not last)
+            act(bl(sZT, b), ind(wt(sW, b, 2), R("SPH")), bias=2048.0, scale=2048.0)
+            if not last:
+                send(R(PL, 24 * b + 8, 24 * b + 16), R("PL%d" % n, 24 * b, 24 * b + 8), 2200)
+            tt(bl("G", 2 * b), ind(R("TT", 0, 256 * b + 256), bl(VL, b, 16, 8)), bl(OM, b), A.mult)
+            tt(bl("G", 2 * b + 1), ind(R("TT", 0, 256 * b + 256), bl(sVL, b, 16, 8)), bl(sOM, b), A.mult)
+            o = R(D[b], 160, 176)
+            for h in range(2):
+                mm(o, bl("G", 2 * b + h), R("G8", 0, 16), h == 0, h == 1)
+            ts(bl("CF", b, 0, 16), o, col(9), A.is_ge, 4096.0, A.mult)
+            tt(bl("XS", b, 0, 16), bl("CF", b, 0, 16), R(PL, 24 * b, 24 * b + 16), A.max)
+            tolist("SM", b, bl("XS", b, 0, 16), R("DUM"), A.min, R(D[b], 176, 192))
+            cp(bl("SL", b, 0, 16), R(D[b], 176, 192))
+            bk = ("P2", "P0")[b]
+            for h, w in ((1, W), (0, sW)):
+                act(bl("GF", 2 * b + h), ind(EW, bl(sVL, b, 0, 8)), scale=col(15 - h))
+                mm(bl(bk, h), R(("DMO", "DME")[h]), bl("EV", b), True, False)
+                mm(bl(bk, h), wt(w, b, 0), R("I"), False, False); mm(bl(bk, h), wt(w, b, 1), R("I7"), False, True)
+            act(bl("PQ", b, 0, 256), R(bk, 0, 256), bias=col(10 + t))
+        for b in range(2):
+            tt(ind(R("E"), bl("SL", b, 0, 16)), bl("GF", b, 0, 256), bl("PQ", b, 0, 256), A.add)
+        act(R("XR"), ind(R("X"), R(sVL, 0, 16)))
         o1 = R("P1", 0, 256)
-        mm(o1, R("G15"), R("FF16"), True, False); mm(o1, R("G15"), R("HUB"), False, not last)
+        mm(o1, R("I"), R("XR"), True, False)
+        for b in range(2):
+            mm(bl("P1", b), bl(sZT, b), R("N32"), False, b == 1)
+        act(R("XN"), o1, AF.Relu, bias=64.0)
         if last:
+            mm(o1, R("I"), R("ZER", 0, 256), True, False)
             for b in range(2):
+                mm(bl("P1", b), wt(sW, b, 0), R("I"), False, False); mm(bl("P1", b), wt(sW, b, 1), R("I7"), False, False)
                 mm(bl("P1", b), bl(sZT, b), R("I"), False, b == 1)
             act(R("YP"), o1, bias=col(24))
             dma(lambda: T.yp[:], lambda: T.YP[15:128:16, :], [], [R("YP")], 2200)
         else:
-            act(R(sF), o1)
+            act(R("NFS"), R(sZT, 0, 256, 16), AF.Relu, bias=2.0, scale=-1.0 / 2048, acc=R("NFC"))
         mm(o1, R("I"), Z, True, False); mm(o1, R("NI"), R("XN"), False, True)
         if last:
             act(R(sZT, 256, 512), o1, AF.Abs)
             dma(lambda s=sZT: T.yz[:], lambda s=sZT: T[s][:, 256:512], [], [R(sZT, 256, 512)], 2200)
-            tt(ind(R("E"), R("SL")), R("GF"), R("PQ"), A.add)
             for c in range(16):
                 mm(R("P2", c, 128, 16), bl("E", c), R("WY"))
             cp(R("YN"), R("P2", 0, 128))
-            mm(R("P0", 0, 128), R("YN"), R("I3"))
+            mm(R("P0", 0, 128), R("YN"), I3)
             cp(R("YT"), R("P0", 0, 128))
             dma(lambda: T.ys[:], lambda: T.YT[:], [], [R("YT")], 2000)
         else:
@@ -445,16 +499,16 @@ def plan(T, g, topo, core, rank):
                 o = bl("P1", b, 256)
                 mm(o, bl(ZT, b, 256), R("I"), True, False); mm(o, bl("XN", b), R("NI"), False, True)
             act(R(sZT, 256, 768), R("P1"), AF.Abs)
-            mm(R("P2", 0, 1), R("C16"), R("NFC"))
-            cp(R("AI", 0, 1), R("P2", 0, 1))
-            ts(R("AI", 1, 2), R("AI", 0, 1), 255, A.bitwise_and)
-            ts(R("ACOL"), R("AI", 1, 2), 32.0, A.mult, -350464.0, A.add)
+            o = R("P2", 0, 1)
+            mm(o, R("C16"), R("NFC"))
+            act(R("AH"), o, bias=129 - 127.5 / 256, scale=1.0 / 256)
+            act(col(26), o, bias=8192.0 * 129 - 350464.0, scale=32.0)
+            act(R("ACOL"), R("AH"), bias=col(26), scale=-8192.0)
             send(R(sVL), R("rVL%d" % n), 2200)
             send(R(sZT, 0, 256), R("rZT%d" % n, 0, 256), 2600)
             send(R(sZT, 256, 768), R("rZT%d" % n, 256, 768), 3100)
-            send(R(sF), R("rF%d" % n), 3000)
+            send(R(sW), R("rW%d" % n), 3500)
             send(R(sOM), R("rOM%d" % n), 3500)
-            tt(ind(R("E"), R("SL")), R("GF"), R("PQ"), A.add)
     return ops, nen * na[0]
 
 
@@ -479,8 +533,16 @@ def schedule(ops):
         o["dep"] = dep
     n = len(ops)
     suc = [[] for _ in range(n)]
+    reach = []
     for i, o in enumerate(ops):
-        o["all"] = set(o["dep"]) | ({o["seq"]} if "seq" in o else set())
+        al = set(o["dep"]) | ({o["seq"]} if "seq" in o else set())
+        far = 0
+        for j in al:
+            far |= reach[j]
+        o["all"] = sorted(j for j in al if not far >> j & 1)
+        for j in al:
+            far |= 1 << j
+        reach.append(far)
         for j in o["all"]:
             suc[j].append(i)
 
@@ -488,34 +550,49 @@ def schedule(ops):
         if j not in ops[i]["dep"]:
             return ops[j]["busy"] - ops[j]["c"]
         return 0.0 if ops[j]["q"] == "p" and ops[i]["q"] == "p" else LAT
+    pred = [o["all"] for o in ops]
+    fw = [[(k, ops[i]["c"] + lat(i, k)) for k in suc[i]] for i in range(n)]
+    bw = [[(k, ops[i]["c"] + lat(k, i)) for k in pred[i]] for i in range(n)]
+    qs = [o["q"] for o in ops]
+    busy = [o["busy"] for o in ops]
+    cost = [o["c"] for o in ops]
+    tail = [o["c"] - o["busy"] for o in ops]
 
-    def place(keyf, pred, succ, back):
-        left = [len(pred[i]) for i in range(n)]
+    def place(keyf, back):
+        left = [len(x) for x in (suc if back else pred)]
         heap = sorted((keyf[i], i) for i in range(n) if left[i] == 0)
         st = [0.0] * n
         rdy = [0.0] * n
-        slots = {}
+        slots = {q: ([], []) for q in ("v", "s", "p", "gq", "y")}
+        edges = bw if back else fw
         while heap:
-            _, i = heap.pop(0)
-            o = ops[i]
+            i = heap.pop(0)[1]
             s = rdy[i]
-            if o["q"]:
-                sl = slots.setdefault(o["q"], [])
-                off = o["c"] - o["busy"] if back else 0.0
+            if qs[i]:
+                sa, sb = slots[qs[i]]
+                off = tail[i] if back else 0.0
+                d = busy[i]
                 s += off
-                k = len(sl)
-                while k > 0 and sl[k - 1][1] > s:
-                    k -= 1
-                while k < len(sl) and sl[k][0] < s + o["busy"]:
-                    s = max(s, sl[k][1])
-                    k += 1
-                sl.insert(k, (s, s + o["busy"]))
+                k = m = len(sa)
+                if k and sb[-1] > s:
+                    lo = 0
+                    while lo < k:
+                        h = (lo + k) // 2
+                        if sb[h] > s:
+                            k = h
+                        else:
+                            lo = h + 1
+                    while k < m and sa[k] < s + d:
+                        if sb[k] > s:
+                            s = sb[k]
+                        k += 1
+                sa.insert(k, s)
+                sb.insert(k, s + d)
                 s -= off
             st[i] = s
-            for k in succ[i]:
-                e = s + o["c"] + (lat(k, i) if back else lat(i, k))
-                if e > rdy[k]:
-                    rdy[k] = e
+            for k, c in edges[i]:
+                if s + c > rdy[k]:
+                    rdy[k] = s + c
                 left[k] -= 1
                 if left[k] == 0:
                     lo, hi, x = 0, len(heap), (keyf[k], k)
@@ -526,36 +603,34 @@ def schedule(ops):
                         else:
                             hi = m
                     heap.insert(lo, x)
-        return st
-    pred = [sorted(o["all"]) for o in ops]
+        return max(st[i] + cost[i] for i in range(n)), st
+
+    def again(key):
+        bk = place(key, True)[1]
+        return place([-(bk[i] + cost[i]) for i in range(n)], False)
+    state = [12345]
+
+    def rnd():
+        state[0] = (state[0] * 1103515245 + 12345) % 2147483648
+        return state[0] / 2147483648.0
     pr = [0.0] * n
     for i in range(n - 1, -1, -1):
-        pr[i] = ops[i]["c"] + max([pr[k] + lat(i, k) for k in suc[i]] + [0.0])
+        pr[i] = cost[i] + max([pr[k] + lat(i, k) for k in suc[i]] + [0.0])
     best = None
-    for it in range(2 * ROUNDS):
-        if it % ROUNDS == 0:
-            key = [-x for x in pr] if it else [float(i) for i in range(n)]
-        st = place(key, pred, suc, False)
-        end = max(st[i] + ops[i]["c"] for i in range(n))
-        if best is None or end < best[0]:
-            best = (end, st)
-        bk = place([-(st[i] + ops[i]["c"]) for i in range(n)], suc, pred, True)
-        key = [-(bk[i] + ops[i]["c"]) for i in range(n)]
-    rs = 12345
+    for key in ([float(i) for i in range(n)], [-x for x in pr]):
+        cur = place(key, False)
+        for it in range(ROUNDS):
+            if best is None or cur[0] < best[0]:
+                best = cur
+            cur = again([-(cur[1][i] + cost[i]) for i in range(n)])
     cur = best
     for it in range(SEARCH):
-        key = []
         amp = (200.0, 600.0, 1500.0)[it % 3]
-        for i in range(n):
-            rs = (rs * 1103515245 + 12345) % 2147483648
-            key.append(-(cur[1][i] + ops[i]["c"]) + amp * (rs / 2147483648.0))
-        bk = place(key, suc, pred, True)
-        st = place([-(bk[i] + ops[i]["c"]) for i in range(n)], pred, suc, False)
-        end = max(st[i] + ops[i]["c"] for i in range(n))
-        if end < cur[0] + 300:
-            cur = (end, st)
-        if end < best[0]:
-            best = (end, st)
+        new = again([-(cur[1][i] + cost[i]) + amp * rnd() for i in range(n)])
+        if new[0] < cur[0] + 300:
+            cur = new
+        if new[0] < best[0]:
+            best = new
     names = {}
     grp = []
     for o in ops:
@@ -566,19 +641,35 @@ def schedule(ops):
     for it in range(GROUPS):
         new = list(off)
         for m in range(1 + it % 2):
-            rs = (rs * 1103515245 + 12345) % 2147483648
-            k = (rs >> 8) % len(names)
-            rs = (rs * 1103515245 + 12345) % 2147483648
-            new[k] += (rs / 2147483648.0 - 0.5) * (8000.0 if it % 3 else 2000.0)
-        st = place([base[i] + new[grp[i]] for i in range(n)], pred, suc, False)
-        end = max(st[i] + ops[i]["c"] for i in range(n))
-        if end <= best[0] + 1:
-            best, off = (end, st), new
-        if it % 250 == 249:
-            base, off = list(best[1]), [0.0] * len(names)
+            new[int(rnd() * len(names))] += (rnd() - 0.5) * (8000.0 if it % 3 else 2000.0)
+        cur = place([base[i] + new[grp[i]] for i in range(n)], False)
+        if cur[0] <= best[0] + 1:
+            best, off = cur, new
+    cur = best
+    for it in range(LOCAL):
+        c0, w = rnd() * cur[0], (1500.0, 4000.0, 9000.0)[it % 3]
+        near = [i for i in range(n) if abs(cur[1][i] - c0) < w]
+        if not near:
+            continue
+        key = list(cur[1])
+        if it % 2:
+            k, d = grp[near[int(rnd() * len(near))]], (rnd() - 0.5) * (1000.0, 4000.0, 10000.0)[it // 6 % 3]
+            for i in near:
+                if grp[i] == k:
+                    key[i] += d
+        else:
+            for i in near:
+                key[i] += (rnd() - 0.5) * (300.0, 1000.0, 3000.0)[it // 6 % 3]
+        new = place(key, False)
+        if it % 4 == 3:
+            new = again([-(new[1][i] + cost[i]) for i in range(n)])
+        if new[0] <= cur[0] + 150.0 * (1 - it / LOCAL):
+            cur = new
+        if new[0] < best[0]:
+            best = new
     st = best[1]
     for i in range(n):
-        ops[i]["t"] = (st[i], st[i] + ops[i]["c"])
+        ops[i]["t"] = (st[i], st[i] + cost[i])
     return sorted(range(n), key=lambda i: (st[i], i))
 
 

import math
from concourse.mybir import AluOpType as A, ActivationFunctionType as AF

HOPS, STEP = 4, 3
F32, BF, F16, I32, U16 = "float32", "bfloat16", "float16", "int32", "uint16"
DIAG = ("I", "NI", "N2I", "BI", "I29", "I21", "N16", "I7", "N7", "N32")
SB = {
    "ENI": (2048, I32), "E": (2560, F32), "X": (2048, BF), "YT": (128, F32), "V0": (16, I32), "WTI": (1, I32),
    "F": (4096, F32), "RW": (4096, BF), "MX": (4096, BF), "RH": (2048, BF),
    "LT": (240, BF), "EXP": (512, BF), "NEX": (512, BF), "Q0": (512, BF), "Q1": (128, F32), "Q3": (128, F32),
    "PI": (8, I32), "COL": (42, F32), "DG": (128 * len(DIAG), BF), "I3": (256, F32), "E0": (128, BF), "AH": (1, BF), "WB": (1, BF),
    "CI0": (256, BF), "CM": (4096, BF), "CW": (384, BF), "W8": (8, BF), "WY": (8, F32), "DMO": (128, F32), "DME": (128, F32),
    "C16": (128, F32), "G8": (64, BF), "KC": (768, BF), "KP": (384, BF), "RS": (384, F32), "DUM": (128, F32),
    "K16": (256, BF), "I16": (128, BF), "IOT": (128, BF), "SPL": (8, U16), "SPH": (8, U16), "V0F": (32, F32),
    "ZER": (256, BF), "M": (48, F32), "HY": (48, F32), "OT": (256, BF), "KI": (384, F32), "GI": (128, F32), "ONE": (128, BF),
    "R32": (256, I32), "RN": (256, I32), "NL": (256, U16), "EV": (256, F32), "RND": (512, F32), "FR": (512, BF), "ST": (256, BF),
    "ENT": (256, F32), "UP": (256, F16), "AL": (256, U16), "VT": (256, BF), "SS": (768, F32), "NFS": (16, BF),
    "UH": (16, BF), "SQ": (16, F32), "QI": (16, I32), "QJ": (32, I32), "FK": (48, F32),
    "RM": (256, F16), "SM": (256, F16), "CF": (32, F32), "XS": (32, F32),
    "LW": (256, BF), "TT": (512, BF), "G": (512, BF), "SL": (32, U16),
    "GF": (512, F32), "PQ": (512, F32), "XN": (256, BF), "XR": (256, BF), "YN": (128, F32), "YP": (256, F32),
}
for _t in range(HOPS):
    SB["PL%d" % _t] = (48, F32)
    for _s in ("r", "s"):
        SB["%sVL%d" % (_s, _t)] = (32, U16)
        SB["%sZT%d" % (_s, _t)] = (768, BF)
        SB["%sOM%d" % (_s, _t)] = (768, BF)
        SB["%sW%d" % (_s, _t)] = (768, BF)
SCRATCH = {k: ("sbuf", [128, v[0]], v[1]) for k, v in SB.items()}
for _b in range(8):
    SCRATCH["P%d" % _b] = ("psum", [128, 512], F32)
SEMAPHORES = ["v", "s", "p", "gq", "sent"] + ["d%d" % i for i in range(11)] + ["a%d" % i for i in range(21)]

CY, PE, LAT, GA, SC = 1.0, 0.5, 140.0, 1.56, 3.5
COM, GROUPS = 800, 200
SEARCH, ROUNDS, LOCAL = 50, 4, 8000
FDVE = ((0, 1, 4, 5), (2, 3, 5), (2, 3, 5), (2, 3, 5))
RDVE = ((0, 5), (), (), ())
MSC = ((), (), (), ())
TTV, STV = False, False
FAIL = 9 * 2 ** 20
MARK = 2048 - 31.0 / 32
NUM = {30: 1.0, 20: 100 * math.log(2.0), 21: 100 * math.log(2.0) + math.log(3.5), 22: 129 - 1023.5 / 2048, 23: 592.0 + 264192,
       24: -2048.0, 33: 32768.0}


def R(n, a=0, b=None, st=1, p0=0, p1=128):
    if n in ("NFC", "ACOL"):
        a = 36 if n == "NFC" else 37
        return ("COL", a, a + 1, 1, 0, 128)
    if n in DIAG:
        o = 128 * DIAG.index(n)
        return ("DG", o + a, o + (128 if b is None else b), st, p0, p1)
    if b is None:
        b = SB[n][0] if n in SB else 512
    return (n, a, b, st, p0, p1)


def plan(T, g, topo, core, rank):
    ops = []
    nx = T.cores[(rank + STEP) % len(T.cores)]
    rid, pid, _ = topo.addr(nx)
    mask = 0
    for e in topo.engines(core, nx)[::2]:
        mask |= 1 << e
    nen = len(topo.engines(core, nx)[::2])

    def ap(r):
        if isinstance(r, (int, float)) or r is None:
            return r
        if r[0] == "ind":
            return ap(r[1]).indirect(ap(r[2]))
        return T[r[0]][r[4]:r[5], r[1]:r[2]:r[3]] if r[3] > 1 else T[r[0]][r[4]:r[5], r[1]:r[2]]

    def flat(rs):
        o = []
        for r in rs:
            if isinstance(r, tuple):
                o += [r[1], r[2]] if r[0] == "ind" else [r]
        return o

    def ne(r):
        return 16 * ne(r[2]) if r[0] == "ind" else (r[2] - r[1] + r[3] - 1) // r[3]

    def two(rs):
        return all(r[0] in SB and SB[r[0]][1] in (BF, F16, U16) for r in rs)

    def add(q, fn, out, ins, cost, sem=None, inc=1, busy=None):
        w = []
        rd = flat(ins)
        for o in out:
            if o[0] == "ind":
                w.append(o[1]); rd.append(o[2])
            else:
                w.append(o)
        ops.append({"q": q, "fn": fn, "w": w, "r": rd, "c": cost, "sem": sem or q, "inc": inc,
                    "busy": cost if busy is None else busy})
        return len(ops) - 1

    def vc(out, a, full, k):
        if out[0] == "ind":
            return 50 + SC * ne(out) * CY
        if a[0] == "ind":
            return 50 + GA * ne(a) * CY
        return 20 + max(64, ne(out) * (k if k else (0.5 if two(full) else 1))) * CY
    V, S, P = g.vector, g.scalar, g.tensor

    def cp(o, a):
        add("v", lambda: V.tensor_copy(ap(o), ap(a)), [o], [a], vc(o, a, [o, a], 0))

    def tt(o, a, b, op):
        add("v", lambda: V.tensor_tensor(ap(o), ap(a), ap(b), op), [o], [a, b],
            vc(o, a, [], 2 if (a[0] in SB and b[0] in SB) else 1))

    def ts(o, a, s1, op0, s2=None, op1=None):
        if op1 is None:
            f = lambda: V.tensor_scalar(ap(o), ap(a), ap(s1), None, op0)
        else:
            f = lambda: V.tensor_scalar(ap(o), ap(a), ap(s1), ap(s2), op0, op1)
        add("v", f, [o], [a, s1, s2], vc(o, a, [o, a], 0))

    def ms(o, c):
        add("v", lambda: V.memset(ap(o), c), [o], [], vc(o, o, [o], 0))

    def scan(o, a, b, init, op0, op1):
        add("v", lambda: V.tensor_tensor_scan(ap(o), ap(a), ap(b), init, op0, op1), [o], [a, b], vc(o, a, [], 1))

    def act(o, a, f=AF.Identity, bias=0.0, scale=1.0, acc=None):
        c = 65 + GA * ne(a) * CY if a[0] == "ind" else 30 + max(64, ne(a)) * CY
        if acc is None:
            fn = lambda: S.activation(ap(o), ap(a), f, bias=ap(bias), scale=ap(scale))
        else:
            fn = lambda: S.activation(ap(o), ap(a), f, bias=ap(bias), scale=ap(scale), accum_out=ap(acc))
        add("s", fn, [o] + ([acc] if acc else []), [a, bias, scale], c + (1300 if f == AF.Exp else 0))

    def mm(o, l, r, start=True, stop=True):
        c = max(min(64, ne(l)), ne(r)) * PE * (4 if SB[l[0]][1] == F32 else 1)
        add("p", lambda: P.matmul(ap(o), ap(l), ap(r), start, stop), [o], [l, r], c)

    def iota(o, pat, base, cm):
        if SB[o[0]][1] == I32:
            f = lambda: g.iota(ap(o), pat, base, cm)
        else:
            f = lambda: g.iota(ap(o), pat, base, cm, allow_small_or_imprecise_dtypes=True)
        add("gq", f, [o], [], 130 + 2 * ne(o) * CY)

    def fill(o, c):
        iota(o, [[0, ne(o)]], c, 0)

    def sel(o, pat, op, c, base, cm):
        add("gq", lambda: g.affine_select(ap(o), ap(o), pat, op, c, base, cm), [o], [o], 170 + 2 * ne(o) * CY)
    nd = [0]

    def dma(o, a, out, ins, cost):
        s = "d%d" % nd[0]
        nd[0] += 1
        add("y", lambda: g.sync.dma_start(o(), a()), out, ins, cost, sem=s, inc=16, busy=60)
        if 1 < nd[0] <= 8:
            ops[-1]["seq"] = len(ops) - 2
    na = [0]

    def send(src, dst, cost):
        cost += COM
        s = "a%d" % na[0]
        na[0] += 1
        i = add("gq", lambda: g.remote_dma(ap(dst), ap(src), T.sem[s], T.sem.sent, pid, rid, mask), [], [src], cost,
                sem="sent", inc=0, busy=300)
        ops.append({"q": None, "w": [dst], "r": [], "c": 0, "sem": s, "inc": nen, "busy": 0, "after": i})

    def ind(w, o):
        return ("ind", w, o)

    def col(j):
        if j in NUM:
            return NUM[j]
        return R("COL", j, j + 1)

    def bl(n, b, off=0, w=128):
        return R(n, off + w * b, off + w * b + w)
    dma(lambda: T.V0[:], lambda: T.v0[:], [R("V0")], [], 2000)
    for c in range(4):
        dma(lambda c=c: T.ENI[:, 512 * c:512 * c + 512], lambda c=c: T.en[:, 512 * c:512 * c + 512],
            [bl("ENI", c, 0, 512)], [], 2800 + 900 * c)
    dma(lambda: T.rZT0[:, 256:512], lambda: T.z0[:], [R("rZT0", 256, 512)], [], 5800)
    dma(lambda: T.WTI[:], lambda: T.wt[:], [R("WTI")], [], 5900)
    dma(lambda: T.X[:], lambda: T.xs[:], [R("X")], [], 7500)
    I3 = R("I3", 0, 128)
    iota(R("PI", 0, 1), [[1, 1]], 0, 1)
    iota(R("KI", 0, 128), [[0, 8], [1, 16]], 0, 0)
    iota(R("Q3"), [[0, 16], [1, 8]], 0, 0)
    iota(R("Q1"), [[1, 128]], 0, -1)
    iota(R("IOT"), [[1, 128]], 0, 0)
    fill(R("rW0", 0, 640), 0)
    iota(R("GI"), [[1, 8], [0, 16]], 0, 0)
    fill(R("ZER"), 0); fill(R("ONE"), 1); fill(R("C16"), 1)
    iota(R("KI", 128, 384), [[0, 16], [1, 16]], 0, 0)
    iota(R("Q0"), [[1, 32], [0, 16]], 0, 0)
    fill(R("RS"), 0); fill(R("RS", 0, 384, 16), 2 ** 24 - 1); fill(R("FK", 32, 48), FAIL)
    for j, c in enumerate((131072, 1040, -129)):
        fill(bl("KP", j), c)
    iota(R("DUM"), [[0, 8], [256, 2], [0, 8]], 2048, 2)
    sel(R("DUM"), [[0, 16], [-16, 8]], A.is_ge, 0.0, 0, 1); sel(R("DUM"), [[0, 16], [16, 8]], A.is_ge, 0.0, 15, -1)
    fill(R("CW"), 65536)
    sel(R("CW"), [[0, 3], [-16, 8], [0, 16]], A.is_ge, 0.0, 0, 1); sel(R("CW"), [[0, 3], [16, 8], [0, 16]], A.is_ge, 0.0, 15, -1)
    sel(R("CW"), [[0, 3], [-1, 128]], A.not_equal, 2.0 ** 24, 0, 1)
    for t in range(HOPS):
        fill(R("sW%d" % t), 0)
    p = R("PI", 0, 1)
    for j, (sh, m) in enumerate(((0, 15), (4, 7), (0, 1), (0, 31), (4, 1), (0, 8))):
        ts(R("PI", j + 1, j + 2), p, sh, A.arith_shift_right, m, A.bitwise_and)
    cp(R("COL", 0, 7), R("PI", 0, 7))
    act(col(18), col(1), AF.Relu, bias=-14.0)
    act(col(14), col(18), bias=col(3), scale=-1.0)
    act(col(15), col(3), bias=col(30), scale=-1.0)
    act(col(16), col(5), scale=128.0)
    ms(col(8), 1e29)
    for t in range(HOPS):
        act(col(10 + t), col(18), scale=2048.0 * (9 + t))
    ts(R("SPL"), R("KI", 0, 8), col(6), A.add)
    ts(R("SPH"), R("KI", 0, 8), 16.0, A.mult, 15.0, A.add)
    ts(I3, R("Q1"), 0.0, A.is_equal)
    for n, c in (("I", 1.0), ("NI", -1.0), ("N2I", -2048.0), ("BI", 8192.0), ("DMO", col(14)), ("DME", col(15)), ("I29", 2.0 ** 29),
                 ("I21", 2.0 ** 21), ("N16", -16.0), ("I7", 128.0), ("N7", -128.0), ("N32", -1.0 / 32)):
        act(R(n), I3, scale=c)
    act(R("E0"), R("ONE"), scale=R("I3", 0, 1))
    ts(R("EXP"), R("Q0"), col(4), A.is_equal)
    if any(MSC):
        act(R("NEX"), R("EXP"), scale=-1.0)
    ts(R("I3", 128, 256), R("GI"), col(2), A.is_equal)
    cp(col(25), R("WTI"))
    ts(R("Q3"), R("Q3"), col(2), A.is_equal)
    act(R("W8"), R("Q3", 0, 8), scale=col(25))
    act(col(17), col(1), bias=col(30))
    act(R("WY"), R("Q3", 0, 8), scale=col(17))
    act(R("G8", 0, 16), R("Q3", 0, 16))
    act(R("G8", 16, 40), R("Q3", 0, 24), scale=8192.0)
    act(R("G8", 40, 64), R("Q3", 0, 24), scale=-4096.0)
    ms(R("CI0"), 2.0 ** -9)
    ms(R("LT"), 0.0); ts(R("LT", 112, 128), R("KI", 0, 16), col(1), A.is_equal)
    act(col(39), R("I3", 1, 2), scale=256.0); act(col(34), R("I3", 0, 1), scale=-7 * 2.0 ** 24)
    act(bl("KC", 0, 0, 384), R("KI"), bias=col(34), scale=col(39))
    act(bl("KC", 1, 0, 384), R("KI"), scale=col(39))
    act(R("K16"), R("KI", 0, 256), bias=col(33), scale=-2048.0)
    act(R("I16"), R("KI", 0, 128))
    act(col(7), col(0), AF.Exp, bias=col(20), scale=-math.log(3.0))
    act(col(9), col(0), AF.Exp, bias=col(21), scale=-math.log(3.0))
    ops[-1]["c"] = ops[-1]["busy"] = 100
    act(col(19), col(8), scale=1e4); act(R("WB"), col(7))
    act(R("ACOL"), col(0), bias=-350464.0, scale=0.0)
    for c in range(4):
        cp(bl("E", c, 0, 512), bl("ENI", c, 0, 512))
    D, K, FM = ("P3", "P4"), ("P5", "P6"), "P7"
    MAG1, MAG2 = 1.5 * 2.0 ** 23, 1.5 * 2.0 ** 31

    def wp(W, b, j, n=1):
        return R(W, 384 * b + 128 * j + 15, 384 * b + 128 * (j + n), 16)

    def wt(W, b, j):
        return R(W, 384 * b + 128 * j, 384 * b + 128 * j + 128)

    def tolist(buf, b, win, mask, op, o):
        tt(bl(buf, b), ind(win, R("SPL")), mask, op)
        for a in range(8):
            mm(o, R("LT", 112 - 16 * a, 240 - 16 * a), R(buf, 128 * b + 16 * a, 128 * b + 16 * a + 16), a == 0, a == 7)

    def table(OM, VL, W, PL, b, base=None, pure=True):
        mm(R(D[b], 136, 144), R("I"), wp(W, b, 0))
        mm(R(D[b], 128, 136), R("I"), wp(W, b, 0), True, False); mm(R(D[b], 128, 136), R("I7"), wp(W, b, 1), False, True)
        if base:
            act(R(PL, 24 * b + 8, 24 * b + 24), R(D[b], 128, 144))
        else:
            act(R(PL, 24 * b, 24 * b + 8), R(D[b], 128, 136))
        tt(bl("OT", b), ind(wt(W, b, 1), R("SPH")), R("I16"), A.is_equal)
        if b == 0:
            act(bl("LW", 0), bl("OT", 0), scale=col(7))
            act(bl("LW", 1), bl("OT", 0), scale=col(19))
        if base:
            tolist("RM", b, R(PL, 24 * b + 8, 24 * b + 24), R("Q3"), A.mult, R(D[b], 144, 160))
            ts(bl(VL, b, 16, 8), R(D[b], 152, 160), col(16), A.add, 256.0 * b, A.add)
            cp(bl(VL, b, 0, 8), R(D[b], 144, 152))
        for c in range(8):
            lo = R(W, 384 * b + 16 * c + 15, 384 * b + 16 * c + 16)
            if b:
                ts(bl("RH", 8 + c), R("IOT"), lo, A.is_equal, R("WB"), A.mult)
            else:
                ts(bl("RH", c), R("IOT"), lo, A.is_equal)
        mm(R(D[b], 384, 512), bl("OT", b), R("I"))
        act(bl(OM, b), R(D[b], 384, 512))
        both = base and pure and not TTV
        bk = FM if b else K[0]

        def sums(bank, c0, l, l0, stop):
            for a in range(4):
                mm(R(bank, c0, c0 + 256, 1, 32 * a, 32 * a + 32), R(l, l0 + 32 * a, l0 + 32 * a + 32),
                   R("RH", 1024 * b + 256 * a, 1024 * b + 256 * a + 256), False, stop)
        first = [bl(base, x, 256, 256) if both or not pure else R("ZER", 0, 256) for x in range(2)]
        if b == 0:
            mm(R(K[0], 0, 256), R("I"), first[0], True, False)
            mm(R(FM, 0, 256), R("I"), first[1], True, False)
        sums(bk, 0, "OT" if b else "LW", 128 * b, True)
        if both or not pure:
            act(bl("TT", b, 0, 256), R(bk, 0, 256))
        if b == 0:
            sums(FM, 0, "LW", 128, False)
        if both:
            if b == 0:
                mm(R(K[0], 256, 512), R("I"), R("ZER", 0, 256), True, False)
            sums(K[0], 256 - 256 * b, "OT" if b else "LW", 128 * b, True)
            act(bl(OM, b, 256, 256), R(K[0], 256 - 256 * b, 512 - 256 * b))
            if b == 0:
                mm(R(K[0], 0, 256), R("I"), R("ZER", 0, 256), True, False)
                sums(K[0], 0, "LW", 128, False)
        elif pure:
            if base:
                tt(bl("TT", b, 0, 256), R(bk, 0, 256), bl(base, b, 256, 256), A.add)
            act(bl(OM, b, 256, 256), R(bk, 0, 256))
    cp(R("rVL0", 0, 16), R("V0"))
    ts(R("QJ", 0, 16), R("V0"), 127, A.bitwise_and); ts(R("QJ", 16, 32), R("V0"), 7, A.arith_shift_right)
    cp(R("V0F"), R("QJ"))
    for j in range(2):
        tolist("RM", j, bl("V0F", j, 0, 16), R("Q3"), A.mult, R(K[j], 0, 16))
        for b in range(2):
            act(wp("rW0", b, j), bl(K[j], b, 0, 8))
    for b in range(2):
        ts(bl("rVL0", b, 16, 8), bl("V0F", b, 0, 8), col(16), A.add, 256.0 * b, A.add)
        table("rOM0", "rVL0", "rW0", "PL0", b)
    for b in range(2):
        mm(bl("P2", b), bl("rZT0", b, 256), R("I"))
    act(R("rZT0", 512, 768), R("P2", 0, 256))

    def spread(src, off, c, neg):
        bk = ("P1", "P2", "P1", "P2", "P0", "P1", "P0", "P1")[c]
        b, q = divmod(c, 4)
        mm(R(bk), R(src, off + 128 * b, off + 128 * b + 128, 1, 32 * q, 32 * q + 32),
           R("NEX" if neg else "EXP", 0, 512, 1, 32 * q, 32 * q + 32), True, not neg)
        return R(bk)
    prev = {}

    def chain(key):
        key = (key, ops[-1]["q"])
        if key in prev:
            ops[-1]["seq"] = prev[key]
        prev[key] = len(ops) - 1
    EW = R("E", 0, 2048)
    for t in range(HOPS):
        last = t == HOPS - 1
        VL, ZT, OM, W, PL = "rVL%d" % t, "rZT%d" % t, "rOM%d" % t, "rW%d" % t, "PL%d" % t
        sVL, sZT, sOM, sW = "sVL%d" % t, "sZT%d" % t, "sOM%d" % t, "sW%d" % t
        n = t + 1
        Z = R(ZT, 256, 512)
        for b in range(2):
            mm(R(FM, b, 16, 2), bl(ZT, b, 256), R("W8"))
        act(R("UH"), R(FM, 0, 16), bias=col(22), scale=1.0 / 2048)
        o = R(FM, 16, 32)
        mm(o, R("N2I"), R("UH"), True, False)
        for b in range(2):
            mm(R(FM, 16 + b, 32, 2), bl(ZT, b, 256), R("W8"), False, b == 1)
        act(R("SQ"), o, AF.Square, bias=col(23))
        ts(R("QI"), R("SQ"), R("ACOL"), A.add)
        ts(R("QJ", 0, 16), R("QI"), 5, A.arith_shift_right, 127, A.bitwise_and)
        ts(R("QJ", 16, 32), R("QI"), 12, A.arith_shift_right, 15, A.bitwise_and)
        ts(R("FK", 0, 32), R("QJ"), float(FAIL), A.add)
        if t:
            mm(R(FM, 0, 256), R("I"), R(ZT, 0, 256), True, False); mm(R(FM, 0, 256), R("NI"), R("K16"), False, True)
            act(R("VT"), R(FM, 0, 256), AF.Relu)
        for b in range(2):
            cp(bl("R32", b), ind(EW if t else R("ENI"), bl(VL, b, 0, 8)))
            ts(bl("RN", b), bl("R32", b), 2047, A.bitwise_and)
            cp(bl("NL", b), bl("RN", b))
        act(R("EV"), ind(EW, R(VL, 0, 16)))
        if t:
            for b in range(2):
                mm(bl("P0", b), bl(ZT, b), R("I"))
        for c in range(8):
            o, a = bl("F", c, 0, 512), ind(EW, bl("NL", c, 0, 32))
            if c in FDVE[t]:
                if t:
                    cp(o, a)
                else:
                    ts(o, a, MARK, A.max, -MARK, A.add)
            elif t:
                act(o, a)
            else:
                act(o, a, AF.Relu, bias=-MARK)
            chain("g")
        for b in range(2):
            o, cc, ent = R(D[b], 0, 256), R(D[b], 0, 128), bl("ENT", b)
            if t:
                for k in range(16):
                    mm(R(D[b], k, 128, 16), R("F", 2048 * b + k, 2048 * b + 2048, 16), R("I3", (k + t) % 16, 128, 16))
                act(ent, cc)
                if STV:
                    ts(bl("ST", b), cc, 1.0 / 2048, A.mult, 129 - 1023.5 / 2048, A.add)
                else:
                    act(bl("ST", b), cc, bias=col(22), scale=1.0 / 2048)
                for k in range(16):
                    s = (2048 * b + k, 2048 * b + 2048, 16)
                    tt(R("CM", *s), R("F", *s), bl("P0", b), A.is_lt)
            else:
                mm(o, R("ONE"), R("CI0"), True, False)
                for k in range(16):
                    mm(R(D[b], k, 256, 16), R("F", 2048 * b + k, 2048 * b + 2048, 16), R("I3", k, 256, 16), False, k == 15)
                ts(bl("RND", b, 0, 256), o, MAG1, A.add, -MAG1, A.add)
                act(bl("ST", b), bl("RND", 2 * b), bias=129 + 1023.5 / 2048, scale=1.0 / 2048)
                act(ent, bl("RND", 2 * b), bias=2047.0)
                tt(bl("FR", b, 0, 256), o, bl("RND", b, 0, 256), A.subtract)
            o = R(D[b], 256, 384)
            mm(o, ent, I3, True, False)
            mm(o, bl("ST", b), R("N2I"), False, True)
            ts(bl("AL", b), o, 264192.0, A.add)
            ts(bl("UP", b), ent, 1.0 / 128, A.mult, 1024 - 63.5 / 128, A.add)
        for b in range(2):
            kb = R(K[b], 0, 384)
            mm(kb, R("ONE"), bl("KC", min(t, 1), 0, 384), True, False)
            if t:
                for k in range(16):
                    mm(R(K[b], k, 384, 16), R("CM", 2048 * b + k, 2048 * b + 2048, 16), R("CW", (k + t) % 16, 384, 16), False, False)
            for j in range(3):
                if t:
                    mm(bl(K[b], j), R("BI"), bl("VT", b), False, False)
                else:
                    mm(bl(K[b], j), R("I29"), bl("FR", 2 * b), False, False)
                    mm(bl(K[b], j), R("I21"), bl("FR", 2 * b + 1), False, False)
            mm(kb, R("E0"), R("KP"), False, False)
            for j, l, r in ((0, I3, "ENT"), (0, R("N7"), "UP"), (1, R("I"), "UP"), (1, R("N16"), "ST"), (2, R("I"), "ST")):
                mm(bl(K[b], j), l, bl(r, b), False, False)
            for c in range(4 * b, 4 * b + 4):
                o, a, x = bl("RW", c, 0, 512), ind(R("X"), bl("AL", c, 0, 32)), bl("MX", c, 0, 512)
                if c in RDVE[t]:
                    cp(o, a)
                else:
                    act(o, a)
                chain("g")
                z = spread(ZT, 512, c, c in MSC[t])
                if c in MSC[t]:
                    mm(z, R("I"), o, False, True)
                    act(x, z, AF.Relu)
                else:
                    tt(x, o, z, A.max)
                chain("c")
            for src in ("RW", "MX"):
                for k in range(16):
                    mm(R(K[b], k, 384, 16), R(src, 2048 * b + k, 2048 * b + 2048, 16),
                       R("G8", 40, 64) if src == "RW" else R("G8", 16, 40), False, src == "MX" and k == 15)
            scan(bl("SS", b, 0, 384), R("RS"), kb, 0.0, A.add, A.min)
            m, hy = bl("M", b, 0, 24), bl("HY", b, 0, 24)
            tt(m, R("SS", 384 * b + 15, 384 * b + 384, 16), R("FK", b, 48, 2), A.min)
            ts(hy, m, MAG2, A.add, -MAG2, A.add)
            tt(wp(sW, b, 0, 3), m, hy, A.subtract)
            table(sOM, sVL, sW, PL, b, OM, not last)
            act(bl(sZT, b), ind(wt(sW, b, 2), R("SPH")), bias=2048.0, scale=2048.0)
            if not last:
                send(R(PL, 24 * b + 8, 24 * b + 16), R("PL%d" % n, 24 * b, 24 * b + 8), 2200)
            tt(bl("G", 2 * b), ind(R("TT", 0, 256 * b + 256), bl(VL, b, 16, 8)), bl(OM, b), A.mult)
            tt(bl("G", 2 * b + 1), ind(R("TT", 0, 256 * b + 256), bl(sVL, b, 16, 8)), bl(sOM, b), A.mult)
            o = R(D[b], 160, 176)
            for h in range(2):
                mm(o, bl("G", 2 * b + h), R("G8", 0, 16), h == 0, h == 1)
            ts(bl("CF", b, 0, 16), o, col(9), A.is_ge, 4096.0, A.mult)
            tt(bl("XS", b, 0, 16), bl("CF", b, 0, 16), R(PL, 24 * b, 24 * b + 16), A.max)
            tolist("SM", b, bl("XS", b, 0, 16), R("DUM"), A.min, R(D[b], 176, 192))
            cp(bl("SL", b, 0, 16), R(D[b], 176, 192))
            bk = ("P2", "P0")[b]
            for h, w in ((1, W), (0, sW)):
                act(bl("GF", 2 * b + h), ind(EW, bl(sVL, b, 0, 8)), scale=col(15 - h))
                mm(bl(bk, h), R(("DMO", "DME")[h]), bl("EV", b), True, False)
                mm(bl(bk, h), wt(w, b, 0), R("I"), False, False); mm(bl(bk, h), wt(w, b, 1), R("I7"), False, True)
            act(bl("PQ", b, 0, 256), R(bk, 0, 256), bias=col(10 + t))
        for b in range(2):
            tt(ind(R("E"), bl("SL", b, 0, 16)), bl("GF", b, 0, 256), bl("PQ", b, 0, 256), A.add)
        act(R("XR"), ind(R("X"), R(sVL, 0, 16)))
        o1 = R("P1", 0, 256)
        mm(o1, R("I"), R("XR"), True, False)
        for b in range(2):
            mm(bl("P1", b), bl(sZT, b), R("N32"), False, b == 1)
        act(R("XN"), o1, AF.Relu, bias=64.0)
        if last:
            mm(o1, R("I"), R("ZER", 0, 256), True, False)
            for b in range(2):
                mm(bl("P1", b), wt(sW, b, 0), R("I"), False, False); mm(bl("P1", b), wt(sW, b, 1), R("I7"), False, False)
                mm(bl("P1", b), bl(sZT, b), R("I"), False, b == 1)
            act(R("YP"), o1, bias=col(24))
            dma(lambda: T.yp[:], lambda: T.YP[15:128:16, :], [], [R("YP")], 2200)
        else:
            act(R("NFS"), R(sZT, 0, 256, 16), AF.Relu, bias=2.0, scale=-1.0 / 2048, acc=R("NFC"))
        mm(o1, R("I"), Z, True, False); mm(o1, R("NI"), R("XN"), False, True)
        if last:
            act(R(sZT, 256, 512), o1, AF.Abs)
            dma(lambda s=sZT: T.yz[:], lambda s=sZT: T[s][:, 256:512], [], [R(sZT, 256, 512)], 2200)
            for c in range(16):
                mm(R("P2", c, 128, 16), bl("E", c), R("WY"))
            cp(R("YN"), R("P2", 0, 128))
            mm(R("P0", 0, 128), R("YN"), I3)
            cp(R("YT"), R("P0", 0, 128))
            dma(lambda: T.ys[:], lambda: T.YT[:], [], [R("YT")], 2000)
        else:
            for b in range(2):
                o = bl("P1", b, 256)
                mm(o, bl(ZT, b, 256), R("I"), True, False); mm(o, bl("XN", b), R("NI"), False, True)
            act(R(sZT, 256, 768), R("P1"), AF.Abs)
            o = R("P2", 0, 1)
            mm(o, R("C16"), R("NFC"))
            act(R("AH"), o, bias=129 - 127.5 / 256, scale=1.0 / 256)
            act(col(26), o, bias=8192.0 * 129 - 350464.0, scale=32.0)
            act(R("ACOL"), R("AH"), bias=col(26), scale=-8192.0)
            send(R(sVL), R("rVL%d" % n), 2200)
            send(R(sZT, 0, 256), R("rZT%d" % n, 0, 256), 2600)
            send(R(sZT, 256, 768), R("rZT%d" % n, 256, 768), 3100)
            send(R(sW), R("rW%d" % n), 3500)
            send(R(sOM), R("rOM%d" % n), 3500)
    return ops, nen * na[0]


def schedule(ops):
    hist = {}
    for i, o in enumerate(ops):
        dep = set()
        if "after" in o:
            dep.add(o["after"])
        for rs, wr in ((o["r"], False), (o["w"], True)):
            for r in rs:
                ps = r[0] not in SB
                a, b, st = (0, 512, 1) if ps else (r[1], r[2], r[3])
                x = wr
                h = hist.setdefault(r[0], [])
                for (j, c, d, y, s2) in h:
                    if j != i and c < b and a < d and (x or y or (ps and ops[j]["q"] != o["q"])) and not (st == s2 and (a - c) % st):
                        dep.add(j)
                if x:
                    h[:] = [e for e in h if not (a <= e[1] and e[2] <= b and (st == 1 or (e[4] == st and a == e[1])))]
                h.append((i, a, b, x, st))
        o["dep"] = dep
    n = len(ops)
    suc = [[] for _ in range(n)]
    reach = []
    for i, o in enumerate(ops):
        al = set(o["dep"]) | ({o["seq"]} if "seq" in o else set())
        far = 0
        for j in al:
            far |= reach[j]
        o["all"] = sorted(j for j in al if not far >> j & 1)
        for j in al:
            far |= 1 << j
        reach.append(far)
        for j in o["all"]:
            suc[j].append(i)

    def lat(j, i):
        if j not in ops[i]["dep"]:
            return ops[j]["busy"] - ops[j]["c"]
        return 0.0 if ops[j]["q"] == "p" and ops[i]["q"] == "p" else LAT
    pred = [o["all"] for o in ops]
    fw = [[(k, ops[i]["c"] + lat(i, k)) for k in suc[i]] for i in range(n)]
    bw = [[(k, ops[i]["c"] + lat(k, i)) for k in pred[i]] for i in range(n)]
    qs = [o["q"] for o in ops]
    busy = [o["busy"] for o in ops]
    cost = [o["c"] for o in ops]
    tail = [o["c"] - o["busy"] for o in ops]

    def place(keyf, back):
        left = [len(x) for x in (suc if back else pred)]
        heap = sorted((keyf[i], i) for i in range(n) if left[i] == 0)
        st = [0.0] * n
        rdy = [0.0] * n
        slots = {q: ([], []) for q in ("v", "s", "p", "gq", "y")}
        edges = bw if back else fw
        while heap:
            i = heap.pop(0)[1]
            s = rdy[i]
            if qs[i]:
                sa, sb = slots[qs[i]]
                off = tail[i] if back else 0.0
                d = busy[i]
                s += off
                k = m = len(sa)
                if k and sb[-1] > s:
                    lo = 0
                    while lo < k:
                        h = (lo + k) // 2
                        if sb[h] > s:
                            k = h
                        else:
                            lo = h + 1
                    while k < m and sa[k] < s + d:
                        if sb[k] > s:
                            s = sb[k]
                        k += 1
                sa.insert(k, s)
                sb.insert(k, s + d)
                s -= off
            st[i] = s
            for k, c in edges[i]:
                if s + c > rdy[k]:
                    rdy[k] = s + c
                left[k] -= 1
                if left[k] == 0:
                    lo, hi, x = 0, len(heap), (keyf[k], k)
                    while lo < hi:
                        m = (lo + hi) // 2
                        if heap[m] < x:
                            lo = m + 1
                        else:
                            hi = m
                    heap.insert(lo, x)
        return max(st[i] + cost[i] for i in range(n)), st

    def again(key):
        bk = place(key, True)[1]
        return place([-(bk[i] + cost[i]) for i in range(n)], False)
    state = [12345]

    def rnd():
        state[0] = (state[0] * 1103515245 + 12345) % 2147483648
        return state[0] / 2147483648.0
    pr = [0.0] * n
    for i in range(n - 1, -1, -1):
        pr[i] = cost[i] + max([pr[k] + lat(i, k) for k in suc[i]] + [0.0])
    best = None
    for key in ([float(i) for i in range(n)], [-x for x in pr]):
        cur = place(key, False)
        for it in range(ROUNDS):
            if best is None or cur[0] < best[0]:
                best = cur
            cur = again([-(cur[1][i] + cost[i]) for i in range(n)])
    cur = best
    for it in range(SEARCH):
        amp = (200.0, 600.0, 1500.0)[it % 3]
        new = again([-(cur[1][i] + cost[i]) + amp * rnd() for i in range(n)])
        if new[0] < cur[0] + 300:
            cur = new
        if new[0] < best[0]:
            best = new
    names = {}
    grp = []
    for o in ops:
        k = (o["q"], (o["w"] or o["r"])[0][0].rstrip("0123"), o["r"][0][0].rstrip("0123") if o["r"] else "", (o["w"] or o["r"])[0][1] >= 128)
        grp.append(names.setdefault(k, len(names)))
    off = [0.0] * len(names)
    base = list(best[1])
    for it in range(GROUPS):
        new = list(off)
        for m in range(1 + it % 2):
            new[int(rnd() * len(names))] += (rnd() - 0.5) * (8000.0 if it % 3 else 2000.0)
        cur = place([base[i] + new[grp[i]] for i in range(n)], False)
        if cur[0] <= best[0] + 1:
            best, off = cur, new
    cur = best
    for it in range(LOCAL):
        c0, w = rnd() * cur[0], (1500.0, 4000.0, 9000.0)[it % 3]
        near = [i for i in range(n) if abs(cur[1][i] - c0) < w]
        if not near:
            continue
        key = list(cur[1])
        if it % 2:
            k, d = grp[near[int(rnd() * len(near))]], (rnd() - 0.5) * (1000.0, 4000.0, 10000.0)[it // 6 % 3]
            for i in near:
                if grp[i] == k:
                    key[i] += d
        else:
            for i in near:
                key[i] += (rnd() - 0.5) * (300.0, 1000.0, 3000.0)[it // 6 % 3]
        new = place(key, False)
        if it % 4 == 3:
            new = again([-(new[1][i] + cost[i]) for i in range(n)])
        if new[0] <= cur[0] + 150.0 * (1 - it / LOCAL):
            cur = new
        if new[0] < best[0]:
            best = new
    st = best[1]
    for i in range(n):
        ops[i]["t"] = (st[i], st[i] + cost[i])
    return sorted(range(n), key=lambda i: (st[i], i))


ORDER = []


def rank_program(g, core, T, topo):
    rank = T.rank_of(core)
    if rank is None:
        return
    ops, sent = plan(T, g, topo, core, rank)
    if not ORDER:
        ORDER.append(schedule(ops))
        ORDER.append([o["dep"] for o in ops])
    Q = {"v": g.vector, "s": g.scalar, "p": g.tensor, "gq": g, "y": g.sync}
    cnt, seen = {}, {}
    for i in ORDER[0]:
        o = ops[i]
        q = o["q"]
        if q:
            need = {}
            for j in ORDER[1][i]:
                d = ops[j]
                if (q == "p" and d["q"] == "p") or d["inc"] == 0:
                    continue
                need[d["sem"]] = max(need.get(d["sem"], 0), d["val"])
            for s in sorted(need):
                if seen.get((q, s), 0) < need[s]:
                    Q[q].wait_ge(T.sem[s], need[s])
                    seen[(q, s)] = need[s]
            ins = o["fn"]()
            if o["inc"]:
                ins.then_inc(T.sem[o["sem"]], o["inc"])
        cnt[o["sem"]] = cnt.get(o["sem"], 0) + o["inc"]
        o["val"] = cnt[o["sem"]]
    cnt["sent"] = sent
    for s in sorted(cnt):
        g.sync.wait_ge(T.sem[s], cnt[s])
